import numpy as np, ml_dtypes
CORES = [2,3,42,43,82,83,122,123]
N = 8
import mx_ref
BF = ml_dtypes.bfloat16
def gentries(a):
    return np.ascontiguousarray(a.reshape(8, 16, -1).transpose(0, 2, 1)).reshape(8, -1)
def gtable(e):
    e = np.asarray(e); return np.ascontiguousarray(e.reshape(8, -1, 16).transpose(0, 2, 1)).reshape(128, -1).astype(np.int32)
def gcols(t, e):
    v = np.concatenate([t.reshape(8, 16, -1, 4), np.zeros((8, 16, 1, 4), BF)], axis=2)
    return np.ascontiguousarray(np.stack([v[g][:, e[g]] for g in range(8)])).reshape(128, -1)
def tile(rs):
    return np.stack(rs, axis=2).reshape(128, -1).astype(BF)
def pick(q, e):
    c = np.concatenate([q[0].reshape(128, -1, 4), np.zeros((128, 1, 4), np.uint8)], axis=1); s = np.concatenate([q[1], np.ones((16, 1), np.uint8)], axis=1)
    return (np.ascontiguousarray(c[:, e].reshape(128, -1)), np.ascontiguousarray(s[:, e]))
def join(*qs):
    return (np.concatenate([q[0] for q in qs], axis=1), np.concatenate([q[1] for q in qs], axis=1))
def put(q, e, v):
    c, s = q[0].reshape(128, -1, 4).copy(), q[1].copy(); c[:, e] = v[0].reshape(128, -1, 4); s[:, e] = v[1]
    return (c.reshape(128, -1), s)
def pk(c, s):
    return (np.ascontiguousarray(c), mx_ref.live(s))
def emit(q):
    return q[0], q[1]
def packed(v, rng):
    q = [mx_ref.quantize(np.ascontiguousarray(v[r])) for r in range(N)]
    return np.stack([a for a, b in q]), np.stack([mx_ref.plane(b, rng) for a, b in q])
def values_of_codes():
    e, c = np.zeros((128, 128, 4), np.float32), np.zeros((128, 2, 4), np.uint8)
    e[np.arange(128), np.arange(128), 0] = 1
    c[:127, :, 0] = np.arange(256).reshape(2, 128).T[:127]
    return mx_ref.matmul(mx_ref.quantize(e.reshape(128, 512).astype(BF)), (c.reshape(128, 8), np.full((16, 2), 127, np.uint8))).T.reshape(-1).astype(np.float64)
CODE_VALUE, SCALE_VALUE = values_of_codes(), 2.0 ** (np.arange(256) - 127.0)
def decode(q):
    return (CODE_VALUE[q[0]].reshape(16, 8, -1, 4) * SCALE_VALUE[q[1]][:, None, :, None] + 0.0).reshape(128, -1).astype(np.float32)
def f(rng, *shape):
    return mx_ref.flush((rng.standard_normal(shape, dtype=np.float32) * np.exp2(rng.integers(-2, 3, shape[:-1] + (1,)))).astype(BF))
def wide(rng, *shape, cols=0):
    v = rng.standard_normal(shape, dtype=np.float32) * np.exp2(rng.integers(-12, 13, shape)).astype(np.float32)
    if cols: v *= np.repeat(np.exp2(rng.integers(-cols, cols + 1, shape[:-2] + (1, shape[-1] // 4))) * (rng.random(shape[:-2] + (1, shape[-1] // 4)) > 0.0625), 4, axis=-1).astype(np.float32)
    return mx_ref.flush(v.astype(BF))
C, HALF = 384, 192
STEP = [1, 2, 4]
def numbers_of(rng):
    return {"x": np.array(f(rng, N, 128, 4 * C)), "lv": np.array(f(rng, N, 128, 4 * C)), "u": np.array(f(rng, N, 128, 512)), "v": np.array(f(rng, N, 128, 512))}
def names(rng):
    return rng.permuted(np.tile(np.arange(2 * C), (N, 8, 1)), axis=2)
def paired(rng, roots):
    p, n = np.flatnonzero(roots), np.flatnonzero(~roots)
    k = np.zeros(2 * C, np.int64)
    k[p] = rng.permutation(n)
    k[np.concatenate([n, np.arange(C, 2 * C)])] = rng.permutation(np.concatenate([p, np.arange(C, 2 * C)]))
    return k
def stored(k):
    return {"lt": np.stack([gtable(k[r][:, :C]) for r in range(N)]), "rt": np.stack([gtable(k[r][:, C:]) for r in range(N)])}
def layers(rng):
    return np.array(f(rng, N, 128, 2048)).reshape(N, 8, 16, 4, 8, 16, 4)
def weights(rng, w):
    c, p = packed(np.ascontiguousarray(w).reshape(N, 128, 2048), rng)
    return {"wc": c, "ws": p}
def setup_inputs(rng):
    return {**numbers_of(rng), **stored(names(rng)), **weights(rng, layers(rng))}
def setup_inputs_ties(rng):
    d = numbers_of(rng)
    o = rng.permutation(N)
    k = rng.integers(-1, 2, (N, 8, 4, C)).astype(np.float32)
    k[o[1]] = 1
    e = names(rng)
    for g in range(8):
        p = rng.permutation(C) < HALF
        k[o[3], g, 0] = np.where(p, 1.0, -1.0)
        if g % 2:
            k[o[3], g, 1] = np.minimum(k[o[3], g, 1], 0)
            k[o[3], g, 2] = k[o[3], g, 0]
        e[o[3], g] = paired(rng, p)
    x = d["x"].reshape(N, 8, 16, C, 4)
    x[:, :, :8] = 0
    x[:, :, :4, :, 0] = k.astype(BF)
    c = np.ones(N, np.float32)
    c[o[0]] = 0
    c[o[2]] = -1
    u = d["u"].reshape(N, 128, 128, 4)
    for g in range(8):
        for h in range(16 * g, 16 * g + 4):
            u[:, :, h] = 0
            u[:, h, h, 0] = c.astype(BF)
    w = layers(rng)
    w[:, :, :, :, :, :8] = 0
    return {"x": x.reshape(N, 128, 4 * C), "lv": d["lv"], "u": u.reshape(N, 128, 512), "v": d["v"], **stored(e), **weights(rng, w)}
def setup_inputs_near(rng):
    d = numbers_of(rng)
    o = rng.permutation(N)
    t = int(np.flatnonzero(o == 0)[0])
    k = np.where(o % 2 == 0, 2.0 ** -30, 1.0).astype(np.float32)
    x = d["x"].astype(np.float32).reshape(N, 8, 16, C, 4)
    lv = d["lv"].astype(np.float32).reshape(N, 8, 16, C, 4)
    s = rng.integers(-1, 2, (N, 8, 4, C)) * np.where(o % 2 == 0, 2.0 ** -28, 1.0)[:, None, None, None]
    x[:, :, :8] = 0
    x[:, :, :4, :, 0] = 1.125 * s
    x[:, :, 4:8, :, 0] = -1.25 * s
    for r in range(N):
        at = [0, C - 1, int(rng.integers(C)), int(rng.integers(C))]
        for g, j in zip(rng.permutation(8)[:4], at): x[r, g, rng.integers(4), j, 0] = 2.0 ** 30 * rng.choice([-1.0, 1.0])
    x[t] = 0
    x[t, :, 7, :, 3] = 2.0 ** -29
    for z in (x, lv):
        z[:, :, 15, :, 3] = 4.0
        z[t, :, 8:] = rng.choice([-1.0, 1.0], (8, 8, C, 4)) * 2.0 ** -26
        z[t, :, 8:12, :, 0] *= np.float32(2.0 ** -4)
        z[t, ::2, 9:12:2, :, 0] = 2.0 ** -30
        z[t, :, 15, :, 3] = 2.0 ** -28
    u = d["u"].reshape(N, 128, 128, 4)
    w = layers(rng)
    w[:, :, :8] = 0
    w[:, :, :, :, :, :8] = 0
    w[:, :, :, 3, :, 15] = 0
    w[:, :, 15, 3, :, 15, 3] = 4.0
    w[t, :, 15, 3, :, 7, 3] = 4.0
    for g in range(8):
        for i in range(4):
            h = 16 * g + i
            u[:, :, h] = 0
            u[:, h, h, 0] = (1.125 * k).astype(BF)
            u[:, h + 4, h, 0] = k.astype(BF)
            u[t, :, h] = 0
            u[t, h, h, 1] = 1.125 * 2.0 ** -30
            u[t, h + 4, h, 1] = 2.0 ** -30
            w[t, g, 8 + i, 1, g, i, 0] = 1.125 * 2.0 ** -5
            w[t, g, 8 + i, 1, g, i + 4, 0] = -1.25 * 2.0 ** -5
    return {"x": x.reshape(N, 128, 4 * C).astype(BF), "lv": lv.reshape(N, 128, 4 * C).astype(BF), "u": u.reshape(N, 128, 512), "v": d["v"], **stored(names(rng)), **weights(rng, w)}
def setup_inputs_odd(rng):
    d = numbers_of(rng)
    x = np.zeros((N, 8, 16, C, 4), np.float32)
    lv = np.zeros((N, 8, 16, C, 4), np.float32)
    a = np.exp2(rng.integers(5, 9, (8, 1)).astype(np.float32))
    b = rng.integers(0, 2, (N, 8, 4, C))
    x[:, :, 0, :, 3] = 1.96875 * 2.0 ** 8
    x[:, :, 0:8:2, :, 0] = (8 + b) * 2.0 ** -8
    x[:, :, 1:8:2, :, 0] = (9 - b) * 2.0 ** -8
    for t in (x, lv):
        t[:, :, 7, :, 1] = 1.125 * a
        t[:, :, 7, :, 2] = 0.0703125 * a
    x[:, :, 9, :, 0] = -a
    u = d["u"].reshape(N, 128, 128, 4)
    w = np.zeros((N, 8, 16, 4, 8, 16, 4), np.float32)
    for g in range(8):
        w[:, g, 7, 0, g, 9, 1] = 28.0
        for i in range(4):
            u[:, :, 16 * g + i] = 0
            u[:, 16 * g + 2 * i, 16 * g + i, 0] = 1.0
            u[:, 16 * g + 2 * i + 1, 16 * g + i, 0] = -1.0
            w[:, g, 7, i, g, 10, 2] = [1.0, 1.25, 0.75, 0.5625][i] * 2.0 ** -5
    return {"x": x.reshape(N, 128, 4 * C).astype(BF), "lv": lv.reshape(N, 128, 4 * C).astype(BF), "u": u.reshape(N, 128, 512), "v": d["v"], **stored(names(rng)), **weights(rng, w.astype(BF))}
def setup_inputs_ends(rng):
    d = numbers_of(rng)
    n = np.arange(N)
    o = np.array([1, 0, 2, 3])[(n & 3) ^ rng.integers(0, 4, 2)[n >> 2]]
    x = np.zeros((N, 8, 16, C, 4), np.float32)
    lv = np.zeros((N, 8, 16, C, 4), np.float32)
    a = np.zeros((N, 8, 4))
    k = names(rng)
    w = np.zeros((N, 128, 4, 128, 4), np.float32)
    i, c = np.arange(128), np.arange(C)
    for r in range(N):
        a[r] = rng.choice([-1.0, 1.0], (8, 4)) * (rng.permutation(8) > 1)[:, None]
        roots = rng.permutation(C) < HALF
        s = rng.choice([-1.0, 1.0], (2, 8, 16, C, 4))
        size = (0.6 + 0.05 * rng.random((2, 8, 16, C, 4))) * 2.0 ** 30
        if o[r] == 0:
            s[:] = -1.0
            k[r] = np.concatenate([2 * C - 1 - c, C - 1 - c])
        if o[r] == 1:
            s[0] = np.where(roots, 1.0, -1.0)[None, None, :, None]
            for g in range(8): k[r, g] = paired(rng, ~roots if a[r, g, 0] < 0 else roots)
        if o[r] == 2: k[r] = np.concatenate([(c + 1) % C, 2 * C - 1 - c])
        if o[r] == 3:
            s[0] = s[0][:, :1, :, :1]
            size[:] = 2.0 ** -28
            for j, g in enumerate(rng.permutation(8)):
                k[r, g] = np.concatenate([rng.permutation(C) + C * (j % 2), rng.permutation(C) + C * (1 - j % 2)])
        x[r], lv[r] = s * size
        if o[r] == 2: w[r] = rng.choice([-1.0, 1.0], (128, 4, 128, 4)) * 2.0 ** -6
        else:
            for b in range(4): w[r, i, b, i, b] = -1.0 if o[r] < 2 else 64.0
    size = np.where(o == 3, 2.0 ** -30, 2.0 ** 30)
    u = d["u"].reshape(N, 128, 128, 4)
    for j in range(4): u[:, :, j::16] = (a[:, :, j] * size[:, None] + 0.0).astype(np.float32).astype(BF)[:, None, :, None]
    v = rng.choice([-1.0, 1.0], (N, 128, 512)) * size[:, None, None]
    return {"x": x.reshape(N, 128, 4 * C).astype(BF), "lv": lv.reshape(N, 128, 4 * C).astype(BF), "u": u.reshape(N, 128, 512), "v": v.astype(np.float32).astype(BF), **stored(k), **weights(rng, w.astype(BF))}
def setup_inputs_spread(rng):
    d = setup_inputs(rng)
    d["x"] = wide(rng, N, 128, 4 * C, cols=6)
    d["lv"] = wide(rng, N, 128, 4 * C, cols=6)
    return d
def check_inputs(d):
    b = []
    for k in ("x", "lv", "u", "v"):
        a = np.abs(d[k].astype(np.float32))
        if not (np.isfinite(a).all() and ((a == 0) | (a >= 2.0 ** -30) & (a <= 2.0 ** 30)).all()): b.append("a value of " + k)
    none, least, most = [emit(mx_ref.quantize(np.full((128, 16), k, np.float32).astype(BF)))[1][0, 0] for k in (0.0, 2.0 ** -6, 2.0 ** 6)]
    for r in range(N):
        if (np.sort(np.concatenate([gentries(d["lt"][r]), gentries(d["rt"][r])], axis=1), axis=1) != np.arange(2 * C)).any(): b.append("lt and rt: not every name once in a group")
        if ((d["wc"][r] == 0x7F) | (d["wc"][r] == 0xFF)).any(): b.append("wc: a code that is no number")
        s = mx_ref.live(d["ws"][r])
        if ((s != none) & ((s < least) | (s > most))).any(): b.append("ws: a scale out of range")
        if (((d["wc"][r].reshape(16, 8, 512, 4) & 0x7F) != 0) & (s == none)[:, None, :, None]).any(): b.append("wc: a code other than zero under the scale of zeros")
    return b
def rewrite(left, right, act, turn):
    g, c = np.nonzero((left < C) & (act > 0) & (np.take_along_axis(act, left % C, 1) < 0))
    s = left[g, c]
    a, b, z = left[g, s], right[g, s], right[g, c]
    t = turn[g, a % C] > 0
    left, right = left.copy(), right.copy()
    left[g, c], right[g, c] = np.where(t, a, s), np.where(t, s, b)
    left[g, s], right[g, s] = np.where(t, b, a), z
    return left, right
def reference(x, lv, u, v, lt, rt, wc, ws):
    qu = [mx_ref.quantize(u[r]) for r in range(N)]
    lay = [pk(wc[r], ws[r]) for r in range(N)]
    left, right = [gentries(lt[r]) for r in range(N)], [gentries(rt[r]) for r in range(N)]
    now, leaf = [x[r] for r in range(N)], [lv[r] for r in range(N)]
    for step in STEP:
        made = []
        for r in range(N):
            s = mx_ref.matmul(qu[r], mx_ref.quantize(now[r])).reshape(8, 16, C)
            for j in range(2): left[r], right[r] = rewrite(left[r], right[r], s[:, 2 * j], s[:, 2 * j + 1])
            win = np.concatenate([now[r], leaf[r]], axis=1)
            z = mx_ref.quantize(((gcols(win, left[r]).astype(np.float32) + gcols(win, right[r]).astype(np.float32)) * np.float32(0.5)).astype(BF))
            made.append(tile([mx_ref.matmul(pick(lay[r], np.arange(128 * b, 128 * b + 128)), z) * np.float32(0.03125) for b in range(4)]))
        for r in range(N):
            p = r ^ step
            m = np.take_along_axis(left[p], right[r] % C, 1) % C
            far = gcols(decode(mx_ref.quantize(made[p])).astype(BF), m[:, :HALF])
            leaf[r] = np.concatenate([far, gcols(made[r], m[:, HALF:])], axis=1)
            now[r] = (now[r].astype(np.float32) + leaf[r].astype(np.float32)).astype(BF)
    y, gr = np.zeros((N, 128, C), np.float32), np.zeros((N, 8, 2 * C), np.float32)
    oc, osc = np.zeros((N, 128, 4 * C), np.uint8), np.zeros((N, 16, C), np.uint8)
    for r in range(N):
        q = mx_ref.quantize(now[r])
        y[r] = mx_ref.matmul(mx_ref.quantize(v[r]), q)
        gr[r] = np.concatenate([left[r], right[r]], axis=1)
        oc[r], osc[r] = emit(q)
    return {"y": y, "gr": gr, "oc": oc, "osc": osc}

@@ -1,0 +1,508 @@
+from concourse.mybir import dt, AluOpType, ActivationFunctionType
+
+C, HALF, STEP = 384, 192, [1, 2, 4]
+OP, ACT = AluOpType, ActivationFunctionType
+RESET, LIFT = -4096.0, 1024.0
+TINY, UP = 2.0 ** -101, 2.0 ** 57
+PAR = TINY * UP
+LONG = 0.25
+WAKE, PATIENCE = 0.1, 0.2
+
+SCRATCH = {}
+PLACE = {}
+
+
+def _sb(n, w, t): SCRATCH[n] = ("sbuf", [128, w], t)
+
+
+def _share(buf, t, items):
+    at = 0
+    for n, w in items:
+        PLACE[n] = (buf, at); at += (w + 7) // 8 * 8
+    _sb(buf, at, t)
+
+
+for _n, _w in (("X0", 1536), ("X1", 1536), ("LV", 1536), ("XYh", 3072), ("H", 1536), ("Z", 1536), ("Rg", 1536), ("F", 768),
+               ("ut", 512), ("vt", 512), ("E", 2048), ("ones", 512), ("sA1", 768), ("sA", C), ("sA2", C), ("tb", C), ("TB1", C), ("TB2", 768),
+               ("oA", 768), ("oB", 768), ("hpF", C), ("GA", C), ("GB", C), ("oS", 768), ("gS", C), ("o2S", C), ("g2S", C), ("d16b", C)):
+    _sb(_n, _w, "bfloat16")
+for _n, _w in (("iotaF", 768), ("imod", 768), ("tiny", C), ("d16n", C), ("d16c", C), ("d4n", C),
+               ("vm", C), ("val", C), ("LPp", 768), ("lpS", C),
+               ("cS", C), ("LD", 768), ("yS", C)):
+    _sb(_n, _w, "float32")
+for _n, _w in (("mF", HALF), ("mS", HALF), ("nF", HALF), ("mnS", HALF), ("d4h", C), ("d16h", C), ("L3h", C), ("R3h", C),
+               ("sR4", C), ("sL4", C), ("s16r", C), ("s16l", C), ("aF", C), ("aS", C)):
+    _sb(_n, _w, "float16")
+_share("wf", "float32", (("cst", 32), ("base", 48), ("n1", 24), ("n16", 24), ("t16", 32), ("u16", 32), ("l2W", 24), ("lcW", 24), ("lcX", 24), ("s1", 24), ("sE", 48), ("A", 24), ("RL", 24), ("KD", 72), ("KD2", 72), ("PK", 48), ("PK2", 24), ("fl2", 48), ("M2", 72), ("TM2", 72), ("bs2", 48), ("AP2", 48), ("AT2", 24), ("hp2", 24), ("hh", 24), ("T2", 24), ("T1", 24),
+                         ("ET", 48), ("HP", 48), ("AT", 48), ("AP", 48), ("bs", 48), ("bl", 24), ("bl2", 24), ("M", 72), ("mA", 24), ("TM", 72), ("sg", 48), ("sg1", 48),
+                         ("mm", 48), ("mo", 48), ("ms", 48)))
+_share("wi", "int32", (("pI", 1), ("p15", 1), ("p3", 1), ("v16", 16), ("v16m", 16), ("v4", 16), ("v4m", 16), ("nI", 24), ("uI", 32)))
+_share("wu", "uint16", [("rU%d" % _k, 24) for _k in range(3)] + [("lU%d" % _k, 24) for _k in range(4)] +
+       [("rU", 24), ("lcU", 24), ("lpU", 24), ("l2U", 24), ("sgU", 48), ("sg1U", 48), ("oR", 96), ("oL", 96), ("mfU", 48), ("mnU", 48), ("uU", 32)])
+_sb("ltI", 24, "int32"); _sb("rtI", 24, "int32")
+for _k in range(3):
+    _sb("LR%d" % _k, 768, "float32"); _sb("LM%d" % _k, 768, "float32")
+    _sb("LP%d" % _k, 768, "float32"); _sb("CP%d" % _k, 768, "float32")
+    _sb("rin%d" % _k, 12, "uint16"); _sb("lin%d" % _k, 24, "uint16")
+    _sb("fq%d" % _k, HALF, "float8_e4m3fn_x4"); _sb("fs%d" % _k, HALF, "uint8")
+    _sb("cin%d" % _k, HALF, "float8_e4m3fn_x4"); _sb("sin%d" % _k, HALF, "uint8")
+_sb("LR3", 768, "float32")
+for _n, _w in (("q_u", 128), ("ul", 512), ("q_v", 128), ("q_e", 512), ("q_w", 512), ("q_x", C), ("q_z", C)):
+    _sb(_n, _w, "float8_e4m3fn_x4"); _sb(_n + "s", _w, "uint8")
+SCRATCH["psS"] = ("psum", [128, 2048], "float32")
+SCRATCH["psH"] = ("psum", [128, 2048], "float32")
+SEMAPHORES = ["cv", "cs", "cp", "cg", "left"] + ["d%d" % _i for _i in range(40)] + ["a%s%d" % (_n, _k) for _n in ("r", "l", "c", "s") for _k in range(3)]
+
+
+def R(n, a, b, st=1, off=None):
+    n, at = PLACE.get(n, (n, 0))
+    return (n, at + a, at + b, st, off)
+
+
+def W(n, a=0): return R(n, a, a + 24)
+
+
+def L16(n, w=C): return R(n, 15, w, 16)
+
+
+def rank_program(g, core, T, topo):
+    rank = T.rank_of(core)
+    if rank is None:
+        return
+    ops = []
+    hist = {}
+    ndma = [0]
+
+    def meet(r, o):
+        if r[0].startswith("ps"): return r[1] // 512 == o[1] // 512
+        if r[2] <= o[1] or o[2] <= r[1]: return False
+        return not (r[3] == o[3] and r[3] > 1 and (r[1] - o[1]) % r[3])
+
+    def add(q, fn, reads, writes, t, sem, n, lat=0.0):
+        i, wait, order = len(ops), set(), set()
+        compute = sem[0] == "c"
+        for isw, rs in ((False, reads), (True, writes)):
+            for r in rs:
+                for w0, o, c in hist.get(r[0], ()):
+                    if not (isw or w0 or r[0].startswith("ps")) or not meet(r, o): continue
+                    if isw and not w0 and compute and ops[c]["q"] == q and ops[c]["sem"] == sem: order.add(c)
+                    else: wait.add(c)
+        ops.append({"q": q, "fn": fn, "wait": wait, "order": order - wait, "t": t, "sem": sem, "n": n, "lat": lat})
+        c = i
+        for r in writes:
+            h = hist.setdefault(r[0], [])
+            if not r[0].startswith("ps"):
+                h[:] = [e for e in h if not (r[3] == 1 and r[1] <= e[1][1] and e[1][2] <= r[2])]
+            else:
+                h[:] = [e for e in h if e[1][1] // 512 != r[1] // 512]
+            h.append((True, r, c))
+        for r in reads: hist.setdefault(r[0], []).append((False, r, c))
+        return i
+
+    def emit():
+        prev = {}
+        for i, o in enumerate(ops):
+            if o["q"] in ("g", "y") or o["q"] in ("v", "s") and o["t"] > LONG:
+                if o["q"] in prev and prev[o["q"]] not in o["wait"]: o["order"].add(prev[o["q"]])
+                prev[o["q"]] = i
+        after = [[] for o in ops]
+        for i, o in enumerate(ops):
+            for c in o["wait"]: after[c].append((i, ops[c]["lat"] + WAKE))
+            for c in o["order"]: after[c].append((i, 0.0))
+        way = [0.0] * len(ops)
+        for i in range(len(ops) - 1, -1, -1): way[i] = ops[i]["t"] + max([0.0] + [d + way[j] for j, d in after[i]])
+        way = [w - i for i, w in enumerate(way)]
+        missing = [len(o["wait"]) + len(o["order"]) for o in ops]
+        ready = [0.0] * len(ops)
+        free, open_ = {}, {}
+        for i, o in enumerate(ops):
+            if not missing[i]: open_.setdefault(o["q"], []).append(i)
+        line = []
+        while any(open_.values()):
+            best = None
+            for q, cand in open_.items():
+                if not cand: continue
+                at = lambda i: ready[i] if q == "far" else max(free.get(q, 0.0), ready[i])
+                t0 = min(at(i) for i in cand)
+                a = max((i for i in cand if at(i) <= t0 + 1e-9), key=lambda i: way[i])
+                b = max((i for i in cand if at(i) <= t0 + PATIENCE * ops[a]["t"]), key=lambda i: way[i])
+                if best is None or at(b) < best[0]: best = (at(b), q, b)
+            t0, q, i = best
+            open_[q].remove(i)
+            line.append(i)
+            end = t0 + ops[i]["t"]
+            free[q] = end
+            for j, d in after[i]:
+                ready[j] = max(ready[j], end + d)
+                missing[j] -= 1
+                if not missing[j]: open_.setdefault(ops[j]["q"], []).append(j)
+        eng = {"v": g.vector, "s": g.scalar, "p": g.tensor, "g": g, "y": g.sync}
+        count = {"left": 0}
+        known = {q: {} for q in eng}
+        for i in line:
+            o = ops[i]
+            q, sem = o["q"], o["sem"]
+            if q == "far":
+                count[sem] = o["n"]
+                o["vc"], o["at"] = {sem: o["n"]}, o["n"]
+                continue
+            need = [ops[c] for c in sorted(o["wait"]) if known[q].get(ops[c]["sem"], 0) < ops[c]["at"]]
+            keep = {}
+            for c in need:
+                if any(d["vc"].get(c["sem"], 0) >= c["at"] and (d["sem"], d["at"]) != (c["sem"], c["at"]) for d in need): continue
+                keep[c["sem"], c["at"]] = c
+            for (s, n), c in keep.items():
+                eng[q].wait_ge(T.sem[s], n)
+                for s, n in c["vc"].items(): known[q][s] = max(known[q].get(s, 0), n)
+            count[sem] = count.get(sem, 0) + o["n"]
+            inst = o["fn"](eng[q])
+            if sem != "left": inst.then_inc(T.sem[sem], o["n"])
+            o["at"] = count[sem]
+            o["vc"] = dict(known[q]); o["vc"][sem] = count[sem]
+        for s in sorted(count): g.wait_ge(T.sem[s], count[s])
+
+    def width(r): return 16 * (r[4][2] - r[4][1]) if r[4] else -(-(r[2] - r[1]) // r[3])
+    def half(*rs): return all(SCRATCH[r[0]][2] in ("bfloat16", "float16", "uint16") for r in rs)
+    def plain(n): return max(64, n) * 0.001
+    def picked(o, a): return 0.06 + width(o) * 0.0035 if o[4] else 0.07 + width(a) * 0.0015
+
+    def run(q, fn, reads, writes, t=1.0):
+        rd = []
+        for r in list(reads) + [r[4] for r in writes if r[4]]:
+            rd.append(r)
+            if r[4]: rd.append(r[4])
+        w = list(writes) + [r for r in rd if r[0].startswith("ps")]
+        rd = [r for r in rd if not r[0].startswith("ps")]
+        add(q, fn, rd, w, t, "c" + q, 1)
+
+    def dma(q, out, in_, reads, writes, lat=2.5):
+        sem = "d%d" % ndma[0]; ndma[0] += 1
+        add(q, lambda e: e.dma_start(out, in_), reads, writes, 0.06, sem, 16, lat)
+
+    def ap(r):
+        n, a, b, st, off = r
+        v = T[n][:, a:b] if st == 1 else T[n][:, a:b:st]
+        if off is not None: v = v.indirect(T[off[0]][:, off[1]:off[2]])
+        return v
+
+    def tt(o, a, b, op):
+        t = picked(o, a) if a[4] else plain(width(o) * (1 if "ps" in (a[0][:2], b[0][:2]) else 2))
+        run("v", lambda e: e.tensor_tensor(ap(o), ap(a), ap(b), op), [a, b], [o], t)
+    def ts(o, a, s1, op0, s2=None, op1=None):
+        rs = [a] + [s for s in (s1, s2) if isinstance(s, tuple)]
+        f = lambda s: ap(s) if isinstance(s, tuple) else s
+        t = plain(width(o) * (0.5 if half(o, a) else 1))
+        if op1 is None: run("v", lambda e: e.tensor_scalar(ap(o), ap(a), f(s1), None, op0), rs, [o], t)
+        else: run("v", lambda e: e.tensor_scalar(ap(o), ap(a), f(s1), f(s2), op0, op1), rs, [o], t)
+    def cp(o, a): run("v", lambda e: e.tensor_copy(ap(o), ap(a)), [a], [o], picked(o, a) if o[4] or a[4] else plain(width(o) * (0.5 if half(o, a) else 1)))
+    def fill(o, c): run("v", lambda e: e.memset(ap(o), c), [], [o], plain(width(o) * (0.5 if half(o) else 1)))
+    def scan(o, d, a): run("v", lambda e: e.tensor_tensor_scan(ap(o), ap(d), ap(a), 0.0, OP.add, OP.max), [d, a], [o], plain(width(o) * (0.5 if half(o, d, a) else 1)))
+    def act(o, a, f, scale=1.0, bias=0.0):
+        kw = {n: x for n, x, d in (("scale", scale, 1.0), ("bias", bias, 0.0)) if x != d}
+        kv = {n: ap(x) if isinstance(x, tuple) else x for n, x in kw.items()}
+        run("s", lambda e: e.activation(ap(o), ap(a), f, **kv), [a] + [x for x in kw.values() if isinstance(x, tuple)], [o], picked(o, a) if a[4] else plain(width(o)))
+    def quant(q, a, b, tile, ta):
+        i = R(tile, 4 * ta, 4 * (ta + b - a))
+        s = q.replace("fq", "fs") if q.startswith("fq") else q + "s"
+        run("v", lambda e: e.quantize_mx(T[q][:, a:b], T[s][:, a:b], ap(i)), [i], [R(q, a, b)], 0.015 + 0.00105 * (b - a))
+    def mm(o, qa, a, qb, b, n, sb=None):
+        s = sb or qb + "s"
+        run("p", lambda e: e.matmul_mx(ap(o), T[qa][:, a:a + 128], T[qa + "s"][:, a:a + 128], T[qb][:, b:b + n], T[s][:, b:b + n], True, True),
+            [R(n_, x, y) for n_, x, y in ((qa, a, a + 128), (qa + "s", a, a + 128), (qb, b, b + n), (s, b, b + n))], [o], (n + 16) * 0.001)
+    def iota(o, pat, base, cm, fl=False):
+        run("g", lambda e: e.iota(ap(o), pat, base, cm, allow_small_or_imprecise_dtypes=True) if fl else e.iota(ap(o), pat, base, cm), [], [o], 0.16 + width(o) * 0.002)
+    def gcopy(o, a, n):
+        run("g", lambda e: e.affine_select(ap(o), ap(a), [[0, n]], OP.is_ge, 0.0, 0, 0), [a], [o], 0.2 + n * 0.002)
+    I15, CORR, CORRC, THH, TE, TT, TEM, TTM, ADD4, TH4, C12, I3, NH2, E2, S2, E2M, S2M, TH16, CORRC1 = [R("cst", i, i + 1) for i in range(19)]
+
+    def remote(dst, out, in_, reads, arr, land, lat):
+        rid, pid, _ = topo.addr(dst)
+        i = add("g", lambda e: e.remote_dma(out, in_, T.sem[arr], T.sem.left, pid, rid, topo.mask(core, dst)), reads, [], 0.8, "left", len(topo.engines(core, dst)))
+        j = add("far", None, [], [land], lat, arr, len(topo.engines(dst, core)))
+        ops[j]["order"] |= {i}
+
+    def load(q, n, src, a, b, bc=None): dma(q, T[n][:, a:b] if bc is None else T[n][:, a:b].bitcast(bc), src, [], [R(n, a, b)])
+    load("s", "ltI", T.lt[:, :], 0, 24)
+    load("y", "X0", T.x[:, :], 0, 1536)
+    load("s", "ut", T.u[:, :], 0, 512)
+    load("s", "rtI", T.rt[:, :], 0, 24)
+    load("y", "LV", T.lv[:, :], 0, 1536)
+    load("y", "q_w", T.wc[:, :], 0, 512, dt.uint8)
+    load("y", "q_ws", T.ws[:, :], 0, 512)
+    load("y", "vt", T.v[:, :], 0, 512)
+
+    iota(R("pI", 0, 1), [[1, 1]], 0, 1)
+    iota(R("v16", 0, 16), [[1, 16]], 128, -1)
+    iota(R("v4", 0, 16), [[-4, 16]], 128, 1)
+    iota(R("nI", 0, 24), [[16, 24]], 0, 0)
+    iota(R("uI", 0, 32), [[1, 4], [16, 8]], 0, 0)
+    iota(R("iotaF", 0, 768), [[1, 768]], 0, 0, True)
+    iota(R("LP0", 0, C), [[0, C]], 400, 0, True)
+    iota(R("CP0", 0, C), [[0, C]], 0, 0, True)
+    fill(R("ones", 0, 512), 1.0)
+    for n in ("sA1", "oA", "oB"): fill(R(n, C, 768), 0.0)
+    for b in range(4):
+        o = R("E", 512 * b, 512 * b + 512)
+        run("g", lambda e, o=o, b=b: e.affine_select(ap(o), T.ones[:, 0:512], [[1, 512]], OP.is_equal, 0.0, -b, -4), [R("ones", 0, 512)], [o])
+    ts(R("p15", 0, 1), R("pI", 0, 1), 15, OP.bitwise_and)
+    ts(R("p3", 0, 1), R("pI", 0, 1), 3, OP.bitwise_and)
+    ts(R("v16m", 0, 16), R("v16", 0, 16), 15, OP.bitwise_and)
+    ts(R("v4m", 0, 16), R("v4", 0, 16), 15, OP.bitwise_and)
+    cp(I15, R("p15", 0, 1)); cp(I3, R("p3", 0, 1))
+    cp(R("uU", 0, 32), R("uI", 0, 32))
+    ts(R("t16", 0, 16), R("v16m", 0, 16), 0.0, OP.is_equal, RESET, OP.mult)
+    ts(R("t16", 16, 32), R("v16m", 0, 16), 1.0, OP.is_equal, LIFT, OP.mult)
+    ts(R("u16", 0, 16), R("v4m", 0, 16), 4.0, OP.is_lt, RESET, OP.mult)
+    ts(R("u16", 16, 32), R("v4m", 0, 16), 12.0, OP.is_ge, LIFT, OP.mult)
+    tt(R("d16n", 0, 16), R("t16", 0, 16), R("t16", 16, 32), OP.add)
+    tt(R("d4n", 0, 16), R("u16", 0, 16), R("u16", 16, 32), OP.add)
+    ts(CORR, I15, 15.0, OP.is_lt, LIFT, OP.mult)
+    ts(C12, I15, 12.0, OP.is_lt, LIFT, OP.mult)
+    w = 16
+    while w < C:
+        m = min(w, C - w)
+        for n in ("d16n", "d4n"): cp(R(n, w, w + m), R(n, 0, m))
+        w += m
+    ts(R("base", 0, 24), R("nI", 0, 24), I15, OP.add)
+    ts(ADD4, C12, -4.0, OP.mult, I3, OP.add)
+    ts(R("n16", 0, 24), R("base", 0, 24), CORR, OP.add)
+    for k, t in ((TH16, 384.0), (TH4, 384.0)): act(k, C12 if k == TH4 else CORR, ACT.Copy, 1.0, t)
+    for k, t in ((THH, 0.5), (TE, -0.5), (TT, -0.875), (TEM, -100.5), (TTM, -100.875),
+                 (E2, -2.0), (S2, -4.0), (E2M, -52.0), (S2M, -54.0)): act(k, CORR, ACT.Copy, 2.0 ** -6, t)
+    act(NH2, CORR, ACT.Copy, -(2.0 ** -6), -2.0)
+    act(CORRC, CORR, ACT.Copy, PAR)
+    act(CORRC1, CORR, ACT.Copy, PAR, PAR)
+    act(R("d16b", 0, C), R("d16n", 0, C), ACT.Copy, 2.0 ** -6)
+    act(R("base", 24, 48), R("base", 0, 24), ACT.Copy, 1.0, 384.0)
+    act(R("n1", 0, 24), R("base", 0, 24), ACT.Identity, PAR, CORRC1)
+    act(R("tiny", 0, C), R("iotaF", 0, C), ACT.Copy, TINY, TINY)
+
+    def parents(k):
+        cp(R("LP%d" % k, 0, 768, 1, W("lU%d" % k)), R("iotaF", 0, C))
+        scan(R("lpS", 0, C), R("d16n", 0, C), R("LP%d" % k, 0, C))
+        ts(W("lpU"), L16("lpS"), CORR, OP.subtract)
+        tt(W("PK", 24), L16("lpS"), W("n16"), OP.subtract)
+
+    def columns():
+        ts(W("lcW"), L16("s16l"), TH16, OP.is_ge, 384.0, OP.mult)
+        tt(W("lcX"), L16("s16l"), W("lcW"), OP.subtract)
+        ts(W("lcU"), W("lcX"), CORR, OP.subtract)
+
+    def structure():
+        offsets_d("KD", L16("s16l"))
+        scan(R("aS", 0, C), R("d16h", 0, C), R("aF", 0, C))
+        tt(W("RL"), L16("s16r"), L16("s16l"), OP.subtract)
+        tt(W("A"), L16("aS"), L16("s16l"), OP.subtract)
+
+    def offsets_d(n, l): tt(W(n), l, W("n16"), OP.subtract)
+
+    def offsets_e(n):
+        act(W(n, 24), W(n), ACT.Copy)
+        act(W(n, 48), W(n), ACT.Copy, -1.0, -384.0)
+
+    cp(W("lU0"), W("ltI")); ts(L16("s16l"), W("ltI"), CORR, OP.add)
+    quant("q_u", 0, 128, "ut", 0)
+    run("s", lambda e: e.activation(T.uls[:, 0:512], T.q_us[:, 0:128].indirect(ap(R("uU", 0, 32))), ACT.Copy), [R("q_u", 0, 128), R("uU", 0, 32)], [R("uls", 0, 512)])
+    run("v", lambda e: e.tensor_copy(T.ul[:, 0:512].bitcast(dt.uint32), T.q_u[:, 0:128].bitcast(dt.uint32).indirect(ap(R("uU", 0, 32)))), [R("q_u", 0, 128), R("uU", 0, 32)], [R("ul", 0, 512)])
+    cp(W("rU"), W("rtI")); ts(L16("s16r"), W("rtI"), CORR, OP.add)
+    act(R("LR0", 0, C), R("iotaF", 0, 768, 1, W("lU0")), ACT.Copy)
+    act(R("LR0", C, 768), R("iotaF", 0, 768, 1, W("rU")), ACT.Copy)
+    act(R("d16h", 0, C), R("d16n", 0, C), ACT.Copy)
+    quant("q_x", 0, C, "X0", 0)
+    parents(0)
+    columns()
+    fill(R("PK", 0, 24), 384.0)
+
+    bank = lambda k, n: R("psS", 512 * k, 512 * k + n)
+
+    def scores(a, b):
+        for k in range(4): mm(bank(k, b - a), "ul", 128 * k, "q_x", a, b - a)
+
+    def sign1(a, b):
+        act(R("sA1", a, b), bank(0, b - a), ACT.Sign)
+        if b == HALF: ts(R("TB1", a, b), bank(1, b - a), 0.0, OP.is_le, 0.25, OP.mult)
+        else:
+            act(R("tb", a, b), bank(1, b - a), ACT.Sign, -1.0, TINY)
+            act(R("TB1", a, b), R("tb", a, b), ACT.Copy, 0.125, 0.125)
+
+    def sign2(a, b):
+        act(R("sA", a, b), bank(2, b - a), ACT.Sign)
+        act(R("TB2", a, b), bank(3, b - a), ACT.Sign, -1.0, TINY)
+        gcopy(R("TB2", C + a, C + b), R("TB2", a, b), b - a)
+        act(R("sA2", a, b), R("sA", a, b), ACT.Copy, 4.0)
+
+    def roots2(a, b): tt(R("vm", a, b), bank(2, b - a), R("tiny", a, b), OP.min)
+    def value2(a, b): act(R("val", a, b), R("vm", a, b), ACT.Relu, UP)
+
+    def roots(kd, gsc, m, tm, bs):
+        tt(W(m, 24), L16(gsc), W("T1"), OP.is_lt)
+        tt(W(m, 48), L16(gsc), W("T2"), OP.is_lt)
+        tt(R(tm, 0, 72), R(m, 0, 72), R(kd, 0, 72), OP.mult)
+        tt(R(bs, 0, 48), R(tm, 0, 48), R("base", 0, 48), OP.add)
+        tt(W(bs, 24), W(bs, 24), W(tm, 48), OP.add)
+
+    for k in range(3):
+        p = T.cores[rank ^ STEP[k]]
+        last = k == 2
+        X, XN = "X%d" % (k % 2), "X%d" % (1 - k % 2)
+        LRk, LMk, LRn, lU = "LR%d" % k, "LM%d" % k, "LR%d" % (k + 1), "lU%d" % k
+        a0, b0 = (0, C) if k == 0 else (0, HALF)
+        scores(a0, b0)
+        if k: structure()
+        sign1(a0, b0)
+        tt(R("oA", 0, C), R("TB1", 0, C, 1, W("lcU")), R("sA1", 0, C), OP.add)
+        act(R("hpF", 0, C), R("sA1", 0, 768, 1, W("lpU")), ACT.Copy, -1.0)
+        act(R("GA", 0, C), R("oA", 0, 768, 1, W(lU)), ACT.Copy)
+        if k == 0: act(R("aF", 0, C), R("LR0", 0, 768, 1, W("lU0")), ACT.Copy)
+        sign2(a0, b0)
+        if k == 0:
+            offsets_d("KD", L16("s16l"))
+            tt(W("RL"), L16("s16r"), L16("s16l"), OP.subtract)
+        offsets_e("KD")
+        if k == 0:
+            act(R("d16c", 0, C), R("d16n", 0, C), ACT.Copy, PAR)
+            act(R("d4h", 0, C), R("d4n", 0, C), ACT.Copy)
+        scan(R("oS", 0, C), R("d16b", 0, C), R("oA", 0, C))
+        scan(R("oS", C, 768), R("d16b", 0, C), R("hpF", 0, C))
+        ts(W("hh"), L16("oS"), THH, OP.is_gt, 100.0, OP.mult)
+        ts(R("ET", 0, 48), L16("oS", 768), TE, OP.is_lt)
+        ts(W("HP"), L16("oS"), TT, OP.is_lt)
+        ts(W("T2"), W("hh"), TTM, OP.add)
+        tt(W("AT", 24), W("ET"), W("ET", 24), OP.mult)
+        tt(W("AT"), W("HP"), W("ET", 24), OP.mult)
+        act(W("T1"), W("hh"), ACT.Identity, 1.0, TEM)
+        scan(R("gS", 0, C), R("d16b", 0, C), R("GA", 0, C))
+        tt(W("bl"), W("AT"), W("RL"), OP.mult)
+        tt(W("bl2"), W("bl"), L16("s16l"), OP.add)
+        if k == 0:
+            scan(R("aS", 0, C), R("d16h", 0, C), R("aF", 0, C))
+            tt(W("A"), L16("aS"), L16("s16l"), OP.subtract)
+        tt(W("M"), L16("gS"), W("T2"), OP.is_lt)
+        tt(W("mA"), W("M"), W("A"), OP.mult)
+        tt(W("l2W"), W("mA"), W("bl2"), OP.add)
+        ts(W("l2U"), W("l2W"), CORR, OP.subtract)
+        if k == 0:
+            ts(R("XYh", 0, 1536), R("X0", 0, 1536), 0.5, OP.mult)
+            ts(R("XYh", 2688, 3072), R("LV", 1152, 1536), 0.5, OP.mult)
+        tt(R("oB", 0, C), R("TB2", 0, 768, 1, W("l2U")), R("sA2", 0, C), OP.add)
+        roots2(a0, b0)
+        if k == 0:
+            iota(R("imod", 0, 768), [[0, 2], [1, 384]], 0, 0, True)
+            for i in (1, 2):
+                iota(R("LP%d" % i, 0, C), [[0, C]], 400, 0, True)
+                iota(R("CP%d" % i, 0, C), [[0, C]], 0, 0, True)
+        if k:
+            for b in range(4):
+                act(R("XYh", 1536 + b, 2304, 4), R("psH", 512 * b, 512 * b + HALF), ACT.Copy, 0.5)
+        act(R("GB", 0, C), R("oB", 0, 768, 1, W("l2U")), ACT.Copy)
+        value2(a0, b0)
+        tt(R("AP", 0, 48), R("AT", 0, 48), R("PK", 0, 48), OP.mult)
+        roots("KD", "gS", "M", "TM", "bs")
+        tt(R("sg1", 0, 48), R("AP", 0, 48), R("bs", 0, 48), OP.add)
+        cp(R("sg1U", 0, 48), R("sg1", 0, 48))
+        scan(R("o2S", 0, C), R("d16b", 0, C), R("oB", 0, C))
+        act(W("s1"), L16("o2S"), ACT.Sign, 1.0, NH2)
+        act(W("T2"), W("s1"), ACT.Identity, 50.0, S2M)
+        act(W("T1"), W("s1"), ACT.Identity, 50.0, E2M)
+        act(W("sE"), L16("o2S"), ACT.Sign, -1.0, S2)
+        act(W("sE", 24), L16("o2S"), ACT.Sign, -1.0, E2)
+        act(W("fl2"), W("sE"), ACT.Relu, 384.0)
+        act(W("fl2", 24), W("sE", 24), ACT.Relu, 1.0 / PAR)
+        act(R(LMk, 0, C), R(LRk, 0, 768, 1, W("sg1U")), ACT.Copy)
+        act(R(LMk, C, 768), R(LRk, 0, 768, 1, W("sg1U", 24)), ACT.Copy)
+        cp(R("CP%d" % k, 0, 768, 1, W("l2U")), R("val", 0, C))
+        offsets_d("KD2", W("l2W"))
+        offsets_e("KD2")
+        if k:
+            for a in (768, 0): act(R("XYh", a, a + 768), R(X, a, a + 768), ACT.Copy, 0.5)
+        else:
+            act(R("XYh", 1536, 2688), R("LV", 0, 1152), ACT.Copy, 0.5)
+        scan(R("g2S", 0, C), R("d16b", 0, C), R("GB", 0, C))
+        tt(W("M2"), L16("g2S"), W("T2"), OP.is_lt)
+        roots("KD2", "g2S", "M2", "TM2", "bs2")
+        scan(R("cS", 0, C), R("d16c", 0, C), R("CP%d" % k, 0, C))
+        ts(W("hp2"), L16("cS"), CORRC, OP.is_gt)
+        tt(W("PK2"), L16("cS"), W("n1"), OP.subtract)
+        tt(W("AP2"), W("fl2"), W("hp2"), OP.mult)
+        tt(W("AT2"), W("fl2", 24), W("hp2"), OP.mult)
+        tt(W("AP2", 24), W("AT2"), W("PK2"), OP.mult)
+        tt(R("sg", 0, 48), R("AP2", 0, 48), R("bs2", 0, 48), OP.add)
+        cp(R("sgU", 0, 48), R("sg", 0, 48))
+        cp(R("R3h", 0, C), R(LMk, 0, 768, 1, W("sgU", 24)))
+        act(R("L3h", 0, C), R(LMk, 0, 768, 1, W("sgU")), ACT.Copy)
+        scan(R("sR4", 0, C), R("d4h", 0, C), R("R3h", 0, C))
+        ts(R("oR", 0, 96), R("sR4", 3, C, 4), 4.0, OP.mult, ADD4, OP.add)
+        PIECES = ((0, 64), (64, 128), (128, 256), (256, 384))
+        for a, b in PIECES:
+            act(R("Rg", 4 * a, 4 * b), R("XYh", 0, 3072, 1, R("oR", a // 4, b // 4)), ACT.Copy)
+        gcopy(R("LD", 0, C), R("L3h", 0, C), C)
+        scan(R("s16r", 0, C), R("d16h", 0, C), R("R3h", 0, C))
+        scan(R("sL4", 0, C), R("d4h", 0, C), R("L3h", 0, C))
+        ts(R("rU%d" % k, 0, 24), L16("s16r"), CORR, OP.subtract)
+        ts(R("oL", 0, 96), R("sL4", 3, C, 4), 4.0, OP.mult, ADD4, OP.add)
+        remote(p, T["rin%d" % k][:, :], ap(R("rU%d" % k, 0, 12)), [R("rU%d" % k, 0, 12)], "ar%d" % k, R("rin%d" % k, 0, 12), 2.2)
+        gcopy(R("LD", C, 768), R("L3h", 0, C), C)
+        scan(R("s16l", 0, C), R("d16h", 0, C), R("L3h", 0, C))
+        ts(W("lU%d" % (k + 1)), L16("s16l"), CORR, OP.subtract)
+        remote(p, T["lin%d" % k][:, :], ap(W("lU%d" % (k + 1))), [W("lU%d" % (k + 1))], "al%d" % k, W("lin%d" % k), 2.2)
+        for c in range(3):
+            for a, b in PIECES:
+                if a // 128 == c: tt(R("Z", 4 * a, 4 * b), R("XYh", 0, 3072, 1, R("oL", a // 4, b // 4)), R("Rg", 4 * a, 4 * b), OP.add)
+            quant("q_z", 128 * c, 128 * c + 128, "Z", 128 * c)
+            for b in range(4):
+                o = R("psH", 512 * b, 512 * b + 128)
+                mm(o, "q_w", 128 * b, "q_z", 128 * c, 128)
+                act(R("H", 512 * c + b, 512 * c + 512, 4), o, ACT.Copy, 0.03125)
+        cp(R("mF", 0, HALF), R("LD", 0, 768, 1, R("rin%d" % k, 0, 12)))
+        scan(R("mS", 0, HALF), R("d4h", 0, HALF), R("mF", 0, HALF))
+        m4 = R("mS", 3, HALF, 4)
+        ts(R("mm", 0, 48), m4, TH4, OP.is_ge, -1536.0, OP.mult)
+        act(R("mo", 0, 48), m4, ACT.Identity, 4.0, ADD4)
+        tt(R("ms", 0, 48), R("mm", 0, 48), R("mo", 0, 48), OP.add)
+        cp(R("mfU", 0, 48), R("ms", 0, 48))
+        cp(R("F", 0, 384), R("H", 0, 1536, 1, R("mfU", 0, 24)))
+        act(R("F", 384, 768), R("H", 0, 1536, 1, R("mfU", 24, 48)), ACT.Copy)
+        quant("fq%d" % k, 0, HALF, "F", 0)
+        remote(p, T["cin%d" % k][:, 0:HALF].bitcast(dt.uint8), T["fq%d" % k][:, 0:HALF].bitcast(dt.uint8), [R("fq%d" % k, 0, HALF)], "ac%d" % k, R("cin%d" % k, 0, HALF), 3.7)
+        remote(p, T["sin%d" % k][:, 0:HALF], T["fs%d" % k][:, 0:HALF], [R("fq%d" % k, 0, HALF)], "as%d" % k, R("sin%d" % k, 0, HALF), 2.7)
+        act(R("LPp", 0, C), R("imod", 0, 768, 1, W("lin%d" % k)), ACT.Copy)
+        act(R("LPp", C, 768), R("imod", 0, 768, 1, W("lin%d" % k)), ACT.Copy)
+        act(R("nF", 0, HALF), R("LPp", 0, 768, 1, R("rU%d" % k, 12, 24)), ACT.Copy)
+        act(R(LRn, C, 768), R(LMk, 0, 768, 1, W("sgU", 24)), ACT.Copy)
+        act(R(LRn, 0, C), R("L3h", 0, C), ACT.Copy)
+        if last: dma("y", T.gr[:, :], T[LRn][0:128:16, :], [R(LRn, 0, 768)], [])
+        if not last: parents(k + 1)
+        scan(R("mnS", 0, HALF), R("d4h", 0, HALF), R("nF", 0, HALF))
+        ts(R("mnU", 0, 48), R("mnS", 3, HALF, 4), 4.0, OP.mult, ADD4, OP.add)
+        tt(R(XN, 768, 1536), R("H", 0, 1536, 1, R("mnU", 0, 48)), R(X, 768, 1536), OP.add)
+        quant("q_x", HALF, C, XN, HALF)
+        if k == 0:
+            quant("q_e", 0, 512, "E", 0)
+            quant("q_v", 0, 128, "vt", 0)
+
+        def finish(a):
+            o = bank(a > 0, HALF)
+            mm(o, "q_v", 0, "q_x", a, HALF)
+            act(R("yS", a, a + HALF), o, ACT.Copy)
+            dma("y", T.oc[:, 4 * a:4 * a + 4 * HALF], T.q_x[:, a:a + HALF].bitcast(dt.uint8), [R("q_x", a, a + HALF)], [])
+            for i in range(4):
+                dma("y", T.osc[4 * i:4 * i + 4, a:a + HALF], T.q_xs[32 * i:32 * i + 4, a:a + HALF], [R("q_x", a, a + HALF)], [])
+            dma("y" if a else "s", T.y[:, a:a + HALF], T.yS[:, a:a + HALF], [R("yS", a, a + HALF)], [])
+        if not last:
+            act(R("XYh", 2304, 3072), R("H", 0, 1536, 1, R("mnU", 0, 48)), ACT.Copy, 0.5)
+            scores(HALF, C)
+            columns()
+            roots2(HALF, C)
+            sign1(HALF, C)
+            sign2(HALF, C)
+            value2(HALF, C)
+            act(R("aF", 0, C), R(LRn, 0, 768, 1, W("lU%d" % (k + 1))), ACT.Copy)
+        else:
+            finish(HALF)
+        for b in range(4):
+            mm(R("psH", 512 * b, 512 * b + HALF), "q_e", 128 * b, "cin%d" % k, 0, HALF, "sin%d" % k)
+        for b in range(4):
+            tt(R(XN, b, 768, 4), R(X, b, 768, 4), R("psH", 512 * b, 512 * b + HALF), OP.add)
+        quant("q_x", 0, HALF, XN, 0)
+        if last: finish(0)
+    emit()

@@ -3,10 +3,10 @@ from concourse.mybir import dt, AluOpType, ActivationFunctionType
 C, HALF, STEP = 384, 192, [1, 2, 4]
 OP, ACT = AluOpType, ActivationFunctionType
 RESET, LIFT = -4096.0, 1024.0
-TINY, UP = 2.0 ** -101, 2.0 ** 57
-PAR = TINY * UP
-LONG = 0.25
-WAKE, PATIENCE = 0.1, 0.2
+TINY = 2.0 ** -101
+MID, NONE0, NONE1 = 192.0, -208.0, -576.0
+CY = 0.00095
+OPT = {"wake": 0.08, "hv": 2, "fsplit": 24, "sflags": 0, "mfs": 1, "far": 3.4, "list": 1.8, "pe": 0.00125, "pieces": (0, 64, 128, 256, 384), "lp": 0, "room": 0.2}
 
 SCRATCH = {}
 PLACE = {}
@@ -23,30 +23,28 @@ def _share(buf, t, items):
 
 
 for _n, _w in (("X0", 1536), ("X1", 1536), ("LV", 1536), ("XYh", 3072), ("H", 1536), ("Z", 1536), ("Rg", 1536), ("F", 768),
-               ("ut", 512), ("vt", 512), ("E", 2048), ("ones", 512), ("sA1", 768), ("sA", C), ("sA2", C), ("tb", C), ("TB1", C), ("TB2", 768),
-               ("oA", 768), ("oB", 768), ("hpF", C), ("GA", C), ("GB", C), ("oS", 768), ("gS", C), ("o2S", C), ("g2S", C), ("d16b", C)):
+               ("ut", 512), ("vt", 512), ("E", 528), ("ones", 528), ("sA1", 16 + C), ("sA2", C), ("TB1", C),
+               ("oT", 2304), ("hpF", C), ("GA", C), ("GB", C), ("oS", 768), ("gS", C), ("s2S", C), ("o2S", C), ("g2S", C),
+               ("d16b", C), ("cval", C)):
     _sb(_n, _w, "bfloat16")
-for _n, _w in (("iotaF", 768), ("imod", 768), ("tiny", C), ("d16n", C), ("d16c", C), ("d4n", C),
-               ("vm", C), ("val", C), ("LPp", 768), ("lpS", C),
-               ("cS", C), ("LD", 768), ("yS", C)):
+for _n, _w in (("iotaF", 768), ("imod", 768), ("LPp", C), ("LM", 768), ("yS", C)):
     _sb(_n, _w, "float32")
 for _n, _w in (("mF", HALF), ("mS", HALF), ("nF", HALF), ("mnS", HALF), ("d4h", C), ("d16h", C), ("L3h", C), ("R3h", C),
-               ("sR4", C), ("sL4", C), ("s16r", C), ("s16l", C), ("aF", C), ("aS", C)):
+               ("sR4", C), ("sL4", C), ("s16", 768), ("aF", C), ("aS", C), ("lpS", C), ("cS", C)):
     _sb(_n, _w, "float16")
-_share("wf", "float32", (("cst", 32), ("base", 48), ("n1", 24), ("n16", 24), ("t16", 32), ("u16", 32), ("l2W", 24), ("lcW", 24), ("lcX", 24), ("s1", 24), ("sE", 48), ("A", 24), ("RL", 24), ("KD", 72), ("KD2", 72), ("PK", 48), ("PK2", 24), ("fl2", 48), ("M2", 72), ("TM2", 72), ("bs2", 48), ("AP2", 48), ("AT2", 24), ("hp2", 24), ("hh", 24), ("T2", 24), ("T1", 24),
-                         ("ET", 48), ("HP", 48), ("AT", 48), ("AP", 48), ("bs", 48), ("bl", 24), ("bl2", 24), ("M", 72), ("mA", 24), ("TM", 72), ("sg", 48), ("sg1", 48),
-                         ("mm", 48), ("mo", 48), ("ms", 48)))
+_share("wf", "float32", (("cst", 32), ("base", 48), ("n16", 24), ("n2", 24), ("t16", 32), ("u16", 32), ("colW", 40), ("colX", 40), ("RL", 24), ("PK", 24), ("x0", 24),
+                         ("ct", 24), ("ca", 24), ("T0", 24), ("N2", 24), ("Tc", 24), ("u1", 24), ("ca1", 24), ("PK1", 24), ("mm", 48), ("mo", 48), ("ms", 48)))
+_share("wh", "float16", (("DA", 120), ("DB", 192), ("DC", 192), ("EB", 192), ("EC", 192), ("EA", 120), ("OA", 120), ("OB", 192), ("OC", 192)))
 _share("wi", "int32", (("pI", 1), ("p15", 1), ("p3", 1), ("v16", 16), ("v16m", 16), ("v4", 16), ("v4m", 16), ("nI", 24), ("uI", 32)))
-_share("wu", "uint16", [("rU%d" % _k, 24) for _k in range(3)] + [("lU%d" % _k, 24) for _k in range(4)] +
-       [("rU", 24), ("lcU", 24), ("lpU", 24), ("l2U", 24), ("sgU", 48), ("sg1U", 48), ("oR", 96), ("oL", 96), ("mfU", 48), ("mnU", 48), ("uU", 32)])
+_share("wu", "uint16", [("rU%d" % _k, 12) for _k in range(3)] + [("lU%d" % _k, 24) for _k in range(4)] +
+       [("rU", 24), ("colU", 40), ("lpU", 24), ("iP", 24), ("iN", 24), ("sgU", 48), ("sg1U", 48), ("oR", 96), ("oL", 96), ("mfU", 48), ("mnU", 48), ("uU", 32)])
 _sb("ltI", 24, "int32"); _sb("rtI", 24, "int32")
 for _k in range(3):
-    _sb("LR%d" % _k, 768, "float32"); _sb("LM%d" % _k, 768, "float32")
-    _sb("LP%d" % _k, 768, "float32"); _sb("CP%d" % _k, 768, "float32")
+    _sb("LP%d" % _k, 768, "bfloat16"); _sb("CP%d" % _k, 1536, "bfloat16")
     _sb("rin%d" % _k, 12, "uint16"); _sb("lin%d" % _k, 24, "uint16")
     _sb("fq%d" % _k, HALF, "float8_e4m3fn_x4"); _sb("fs%d" % _k, HALF, "uint8")
     _sb("cin%d" % _k, HALF, "float8_e4m3fn_x4"); _sb("sin%d" % _k, HALF, "uint8")
-_sb("LR3", 768, "float32")
+for _k in range(4): _sb("LR%d" % _k, 3 * C, "float32")
 for _n, _w in (("q_u", 128), ("ul", 512), ("q_v", 128), ("q_e", 512), ("q_w", 512), ("q_x", C), ("q_z", C)):
     _sb(_n, _w, "float8_e4m3fn_x4"); _sb(_n + "s", _w, "uint8")
 SCRATCH["psS"] = ("psum", [128, 2048], "float32")
@@ -62,7 +60,10 @@ def R(n, a, b, st=1, off=None):
 def W(n, a=0): return R(n, a, a + 24)
 
 
-def L16(n, w=C): return R(n, 15, w, 16)
+def L16(n, a=0, b=C): return R(n, a + 15, b, 16)
+
+
+def slot(n, s, of=4, a=0, k=24): return R(n, of * a + s, of * (a + k), of)
 
 
 def rank_program(g, core, T, topo):
@@ -72,6 +73,7 @@ def rank_program(g, core, T, topo):
     ops = []
     hist = {}
     ndma = [0]
+    WAKE = OPT["wake"]
 
     def meet(r, o):
         if r[0].startswith("ps"): return r[1] // 512 == o[1] // 512
@@ -100,47 +102,22 @@ def rank_program(g, core, T, topo):
         return i
 
     def emit():
-        prev = {}
-        for i, o in enumerate(ops):
-            if o["q"] in ("g", "y") or o["q"] in ("v", "s") and o["t"] > LONG:
-                if o["q"] in prev and prev[o["q"]] not in o["wait"]: o["order"].add(prev[o["q"]])
-                prev[o["q"]] = i
-        after = [[] for o in ops]
-        for i, o in enumerate(ops):
-            for c in o["wait"]: after[c].append((i, ops[c]["lat"] + WAKE))
-            for c in o["order"]: after[c].append((i, 0.0))
-        way = [0.0] * len(ops)
-        for i in range(len(ops) - 1, -1, -1): way[i] = ops[i]["t"] + max([0.0] + [d + way[j] for j, d in after[i]])
-        way = [w - i for i, w in enumerate(way)]
-        missing = [len(o["wait"]) + len(o["order"]) for o in ops]
-        ready = [0.0] * len(ops)
-        free, open_ = {}, {}
-        for i, o in enumerate(ops):
-            if not missing[i]: open_.setdefault(o["q"], []).append(i)
-        line = []
-        while any(open_.values()):
-            best = None
-            for q, cand in open_.items():
-                if not cand: continue
-                at = lambda i: ready[i] if q == "far" else max(free.get(q, 0.0), ready[i])
-                t0 = min(at(i) for i in cand)
-                a = max((i for i in cand if at(i) <= t0 + 1e-9), key=lambda i: way[i])
-                b = max((i for i in cand if at(i) <= t0 + PATIENCE * ops[a]["t"]), key=lambda i: way[i])
-                if best is None or at(b) < best[0]: best = (at(b), q, b)
-            t0, q, i = best
-            open_[q].remove(i)
-            line.append(i)
-            end = t0 + ops[i]["t"]
-            free[q] = end
-            for j, d in after[i]:
-                ready[j] = max(ready[j], end + d)
-                missing[j] -= 1
-                if not missing[j]: open_.setdefault(ops[j]["q"], []).append(j)
+        busy = {}
+        for o in ops:
+            t0 = max([0.0] + [ops[c]["end"] + ops[c]["lat"] + WAKE for c in o["wait"]] + [ops[c]["end"] for c in o["order"]])
+            if o["q"] != "far":
+                held = busy.setdefault(o["q"], [])
+                n = 0
+                for n, (x, y) in enumerate(held + [(1e9, 1e9)]):
+                    if t0 + o["t"] * (1 - OPT["room"]) <= x + 1e-9 and t0 < x: break
+                    t0 = max(t0, y)
+                held.insert(n, (t0, t0 + o["t"]))
+            o["start"], o["end"] = t0, t0 + o["t"]
+        OPT["est"] = max(o["end"] + o["lat"] for o in ops)
         eng = {"v": g.vector, "s": g.scalar, "p": g.tensor, "g": g, "y": g.sync}
         count = {"left": 0}
         known = {q: {} for q in eng}
-        for i in line:
-            o = ops[i]
+        for o in sorted(ops, key=lambda o: o["start"]):
             q, sem = o["q"], o["sem"]
             if q == "far":
                 count[sem] = o["n"]
@@ -163,8 +140,8 @@ def rank_program(g, core, T, topo):
 
     def width(r): return 16 * (r[4][2] - r[4][1]) if r[4] else -(-(r[2] - r[1]) // r[3])
     def half(*rs): return all(SCRATCH[r[0]][2] in ("bfloat16", "float16", "uint16") for r in rs)
-    def plain(n): return max(64, n) * 0.001
-    def picked(o, a): return 0.06 + width(o) * 0.0035 if o[4] else 0.07 + width(a) * 0.0015
+    def plain(n): return max(64, n) * CY
+    def picked(o, a): return 0.05 + width(o) * 3.8 * CY if o[4] else 0.06 + width(a) * 1.56 * CY
 
     def run(q, fn, reads, writes, t=1.0):
         rd = []
@@ -175,9 +152,9 @@ def rank_program(g, core, T, topo):
         rd = [r for r in rd if not r[0].startswith("ps")]
         add(q, fn, rd, w, t, "c" + q, 1)
 
-    def dma(q, out, in_, reads, writes, lat=2.5):
+    def dma(q, out, in_, reads, writes, lat=2.0, hold=0.06, **kw):
         sem = "d%d" % ndma[0]; ndma[0] += 1
-        add(q, lambda e: e.dma_start(out, in_), reads, writes, 0.06, sem, 16, lat)
+        add(q, lambda e: e.dma_start(out, in_, **kw), reads, writes, hold, sem, 16, lat)
 
     def ap(r):
         n, a, b, st, off = r
@@ -196,122 +173,123 @@ def rank_program(g, core, T, topo):
         else: run("v", lambda e: e.tensor_scalar(ap(o), ap(a), f(s1), f(s2), op0, op1), rs, [o], t)
     def cp(o, a): run("v", lambda e: e.tensor_copy(ap(o), ap(a)), [a], [o], picked(o, a) if o[4] or a[4] else plain(width(o) * (0.5 if half(o, a) else 1)))
     def fill(o, c): run("v", lambda e: e.memset(ap(o), c), [], [o], plain(width(o) * (0.5 if half(o) else 1)))
-    def scan(o, d, a): run("v", lambda e: e.tensor_tensor_scan(ap(o), ap(d), ap(a), 0.0, OP.add, OP.max), [d, a], [o], plain(width(o) * (0.5 if half(o, d, a) else 1)))
+    def scan(o, d, a, first=0.0, op0=OP.add, op1=OP.max):
+        run("v", lambda e: e.tensor_tensor_scan(ap(o), ap(d), ap(a), first, op0, op1), [d, a], [o], plain(width(o) * (0.5 if half(o, d, a) else 1)))
+    def chain(o, d, a, n): scan(R(o, 0, n), R(d, 0, n), R(a, 0, n), 0.0, OP.mult, OP.add)
     def act(o, a, f, scale=1.0, bias=0.0):
         kw = {n: x for n, x, d in (("scale", scale, 1.0), ("bias", bias, 0.0)) if x != d}
         kv = {n: ap(x) if isinstance(x, tuple) else x for n, x in kw.items()}
         run("s", lambda e: e.activation(ap(o), ap(a), f, **kv), [a] + [x for x in kw.values() if isinstance(x, tuple)], [o], picked(o, a) if a[4] else plain(width(o)))
-    def quant(q, a, b, tile, ta):
-        i = R(tile, 4 * ta, 4 * (ta + b - a))
+    def pick(on_scalar, o, a): act(o, a, ACT.Copy) if on_scalar else cp(o, a)
+    def sfill(o, c): act(o, R("ones", 0, width(o)), ACT.Copy, c)
+    def quant(q, a, b, tile, ta, shift=0):
+        i = R(tile, 4 * ta + shift, 4 * (ta + b - a) + shift)
         s = q.replace("fq", "fs") if q.startswith("fq") else q + "s"
-        run("v", lambda e: e.quantize_mx(T[q][:, a:b], T[s][:, a:b], ap(i)), [i], [R(q, a, b)], 0.015 + 0.00105 * (b - a))
+        run("v", lambda e: e.quantize_mx(T[q][:, a:b], T[s][:, a:b], ap(i)), [i], [R(q, a, b)], 0.015 + 0.001 * (b - a))
     def mm(o, qa, a, qb, b, n, sb=None):
         s = sb or qb + "s"
         run("p", lambda e: e.matmul_mx(ap(o), T[qa][:, a:a + 128], T[qa + "s"][:, a:a + 128], T[qb][:, b:b + n], T[s][:, b:b + n], True, True),
-            [R(n_, x, y) for n_, x, y in ((qa, a, a + 128), (qa + "s", a, a + 128), (qb, b, b + n), (s, b, b + n))], [o], (n + 16) * 0.001)
+            [R(n_, x, y) for n_, x, y in ((qa, a, a + 128), (qa + "s", a, a + 128), (qb, b, b + n), (s, b, b + n))], [o], (n + 16) * OPT["pe"])
     def iota(o, pat, base, cm, fl=False):
-        run("g", lambda e: e.iota(ap(o), pat, base, cm, allow_small_or_imprecise_dtypes=True) if fl else e.iota(ap(o), pat, base, cm), [], [o], 0.16 + width(o) * 0.002)
-    def gcopy(o, a, n):
-        run("g", lambda e: e.affine_select(ap(o), ap(a), [[0, n]], OP.is_ge, 0.0, 0, 0), [a], [o], 0.2 + n * 0.002)
-    I15, CORR, CORRC, THH, TE, TT, TEM, TTM, ADD4, TH4, C12, I3, NH2, E2, S2, E2M, S2M, TH16, CORRC1 = [R("cst", i, i + 1) for i in range(19)]
+        run("g", lambda e: e.iota(ap(o), pat, base, cm, allow_small_or_imprecise_dtypes=True) if fl else e.iota(ap(o), pat, base, cm), [], [o], 0.15 + width(o) * 2 * CY)
+    def gfill(o, c): iota(o, [[0, width(o)]], int(c), 0, True)
+    def gcopy(o, a):
+        run("g", lambda e: e.affine_select(ap(o), ap(a), [[0, width(o)]], OP.is_ge, 0.0, 0, 0), [a], [o], 0.2 + width(o) * 2 * CY)
+    I15, I3, CORR, C12, ADD4, TH4, TH16, KAP, NKAP, KLO, XA, GB0, KS, LPC, UC, KT, X4, X384 = [R("cst", i, i + 1) for i in range(18)]
 
-    def remote(dst, out, in_, reads, arr, land, lat):
+    def lane(k, a, b): act(k, CORR, ACT.Copy, a, b)
+
+    def remote(dst, out, in_, reads, arr, land, lat, part=None):
         rid, pid, _ = topo.addr(dst)
-        i = add("g", lambda e: e.remote_dma(out, in_, T.sem[arr], T.sem.left, pid, rid, topo.mask(core, dst)), reads, [], 0.8, "left", len(topo.engines(core, dst)))
-        j = add("far", None, [], [land], lat, arr, len(topo.engines(dst, core)))
+        es = topo.engines(core, dst)
+        if part is not None: es = es[part * len(es) // 2:(part + 1) * len(es) // 2]
+        i = add("g", lambda e: e.remote_dma(out, in_, T.sem[arr], T.sem.left, pid, rid, sum(1 << n for n in es)), reads, [], 0.6, "left", len(es))
+        j = add("far", None, [], [land], lat, arr, len(es))
         ops[j]["order"] |= {i}
 
-    def load(q, n, src, a, b, bc=None): dma(q, T[n][:, a:b] if bc is None else T[n][:, a:b].bitcast(bc), src, [], [R(n, a, b)])
+    def load(q, n, src, a, b, bc=None, behind=(), lat=1.7):
+        dma(q, T[n][:, a:b] if bc is None else T[n][:, a:b].bitcast(bc), src, list(behind), [R(n, a, b)], lat)
+    load("y", "ut", T.u[:, :], 0, 512, lat=1.9)
     load("s", "ltI", T.lt[:, :], 0, 24)
-    load("y", "X0", T.x[:, :], 0, 1536)
-    load("s", "ut", T.u[:, :], 0, 512)
+    load("y", "X0", T.x[:, :], 0, 1536, lat=3.0)
     load("s", "rtI", T.rt[:, :], 0, 24)
-    load("y", "LV", T.lv[:, :], 0, 1536)
-    load("y", "q_w", T.wc[:, :], 0, 512, dt.uint8)
-    load("y", "q_ws", T.ws[:, :], 0, 512)
-    load("y", "vt", T.v[:, :], 0, 512)
+    load("y", "LV", T.lv[:, :], 0, 1536, None, [R("ut", 0, 512)], 3.0)
+    load("y", "q_w", T.wc[:, :], 0, 512, dt.uint8, [R("X0", 0, 1536)], 3.0)
+    load("y", "q_ws", T.ws[:, :], 0, 512, None, [R("X0", 0, 1536)], 3.0)
+    load("y", "vt", T.v[:, :], 0, 512, None, [R("X0", 0, 1536)], 3.0)
 
+    iota(R("uI", 0, 32), [[1, 4], [16, 8]], 0, 0)
+    cp(R("uU", 0, 32), R("uI", 0, 32))
+    quant("q_u", 0, 128, "ut", 0)
+    for a in (0, 256):
+        o = R("uU", a // 16, a // 16 + 16)
+        run("s", lambda e, a=a, o=o: e.activation(T.uls[:, a:a + 256], T.q_us[:, 0:128].indirect(ap(o)), ACT.Copy), [R("q_u", 0, 128), o], [R("uls", a, a + 256)], 0.45)
+        run("v", lambda e, a=a, o=o: e.tensor_copy(T.ul[:, a:a + 256].bitcast(dt.uint32), T.q_u[:, 0:128].bitcast(dt.uint32).indirect(ap(o))), [R("q_u", 0, 128), o], [R("ul", a, a + 256)], 0.45)
+    quant("q_x", 0, C, "X0", 0)
+
+    def widen(n):
+        w = 16
+        while w < C:
+            m = min(w, C - w)
+            cp(R(n, w, w + m), R(n, 0, m))
+            w += m
     iota(R("pI", 0, 1), [[1, 1]], 0, 1)
     iota(R("v16", 0, 16), [[1, 16]], 128, -1)
-    iota(R("v4", 0, 16), [[-4, 16]], 128, 1)
     iota(R("nI", 0, 24), [[16, 24]], 0, 0)
-    iota(R("uI", 0, 32), [[1, 4], [16, 8]], 0, 0)
+    iota(R("v4", 0, 16), [[-4, 16]], 128, 1)
     iota(R("iotaF", 0, 768), [[1, 768]], 0, 0, True)
-    iota(R("LP0", 0, C), [[0, C]], 400, 0, True)
-    iota(R("CP0", 0, C), [[0, C]], 0, 0, True)
-    fill(R("ones", 0, 512), 1.0)
-    for n in ("sA1", "oA", "oB"): fill(R(n, C, 768), 0.0)
-    for b in range(4):
-        o = R("E", 512 * b, 512 * b + 512)
-        run("g", lambda e, o=o, b=b: e.affine_select(ap(o), T.ones[:, 0:512], [[1, 512]], OP.is_equal, 0.0, -b, -4), [R("ones", 0, 512)], [o])
+    gfill(R("oT", C, 1536), 0)
+    gfill(R("CP0", 0, C), NONE1)
+    fill(R("ones", 0, 528), 1.0)
+    fill(R("LP0", 0, C), NONE0)
+    scan(R("cval", 0, C), R("ones", 0, C), R("ones", 0, C), -MID - 1, OP.add, OP.mult)
     ts(R("p15", 0, 1), R("pI", 0, 1), 15, OP.bitwise_and)
-    ts(R("p3", 0, 1), R("pI", 0, 1), 3, OP.bitwise_and)
+    cp(I15, R("p15", 0, 1))
+    ts(CORR, I15, 15.0, OP.is_lt, LIFT, OP.mult)
     ts(R("v16m", 0, 16), R("v16", 0, 16), 15, OP.bitwise_and)
-    ts(R("v4m", 0, 16), R("v4", 0, 16), 15, OP.bitwise_and)
-    cp(I15, R("p15", 0, 1)); cp(I3, R("p3", 0, 1))
-    cp(R("uU", 0, 32), R("uI", 0, 32))
     ts(R("t16", 0, 16), R("v16m", 0, 16), 0.0, OP.is_equal, RESET, OP.mult)
     ts(R("t16", 16, 32), R("v16m", 0, 16), 1.0, OP.is_equal, LIFT, OP.mult)
-    ts(R("u16", 0, 16), R("v4m", 0, 16), 4.0, OP.is_lt, RESET, OP.mult)
-    ts(R("u16", 16, 32), R("v4m", 0, 16), 12.0, OP.is_ge, LIFT, OP.mult)
-    tt(R("d16n", 0, 16), R("t16", 0, 16), R("t16", 16, 32), OP.add)
-    tt(R("d4n", 0, 16), R("u16", 0, 16), R("u16", 16, 32), OP.add)
-    ts(CORR, I15, 15.0, OP.is_lt, LIFT, OP.mult)
-    ts(C12, I15, 12.0, OP.is_lt, LIFT, OP.mult)
-    w = 16
-    while w < C:
-        m = min(w, C - w)
-        for n in ("d16n", "d4n"): cp(R(n, w, w + m), R(n, 0, m))
-        w += m
+    tt(R("d16h", 0, 16), R("t16", 0, 16), R("t16", 16, 32), OP.add)
     ts(R("base", 0, 24), R("nI", 0, 24), I15, OP.add)
-    ts(ADD4, C12, -4.0, OP.mult, I3, OP.add)
-    ts(R("n16", 0, 24), R("base", 0, 24), CORR, OP.add)
-    for k, t in ((TH16, 384.0), (TH4, 384.0)): act(k, C12 if k == TH4 else CORR, ACT.Copy, 1.0, t)
-    for k, t in ((THH, 0.5), (TE, -0.5), (TT, -0.875), (TEM, -100.5), (TTM, -100.875),
-                 (E2, -2.0), (S2, -4.0), (E2M, -52.0), (S2M, -54.0)): act(k, CORR, ACT.Copy, 2.0 ** -6, t)
-    act(NH2, CORR, ACT.Copy, -(2.0 ** -6), -2.0)
-    act(CORRC, CORR, ACT.Copy, PAR)
-    act(CORRC1, CORR, ACT.Copy, PAR, PAR)
-    act(R("d16b", 0, C), R("d16n", 0, C), ACT.Copy, 2.0 ** -6)
-    act(R("base", 24, 48), R("base", 0, 24), ACT.Copy, 1.0, 384.0)
-    act(R("n1", 0, 24), R("base", 0, 24), ACT.Identity, PAR, CORRC1)
-    act(R("tiny", 0, C), R("iotaF", 0, C), ACT.Copy, TINY, TINY)
+    widen("d16h")
+    for k, t in ((TH16, 384.0), (LPC, NONE0), (UC, NONE1)): lane(k, 1.0, t)
+    act(W("n16"), W("base"), ACT.Identity, 1.0, CORR)
+    act(W("n2"), W("n16"), ACT.Copy, 1.0, -MID)
+    act(W("base", 24), W("base"), ACT.Copy, 1.0, 384.0)
+    sfill(R("sA1", 0, 16), 0.0)
+    sfill(R("DA", 0, 504), 1.0)
+    act(R("d16b", 0, C), R("d16h", 0, C), ACT.Copy, 2.0 ** -6)
+    for k, a, b in ((KAP, 1, 0.0), (NKAP, -1, 0.0), (KLO, 1, -0.5), (XA, 2, -1.5), (GB0, -1, -0.75), (KS, 768, 0.0), (KT, 100, 50.0),
+                    (X4, 8, -7.0), (X384, 8 * 384, -7.0 * 384)): lane(k, a * 2.0 ** -6, b)
+    sfill(slot("DA", 0, 5), 0.0)
+    sfill(slot("DB", 0, 4, 0, 96), 0.0)
+    sfill(slot("EB", 2, 4, 0, 96), 0.0)
+    for n in ("EB", "EC"): act(slot(n, 3, 4, 0, 48), R("base", 0, 48), ACT.Copy)
+
+    SL, SR = L16("s16", C, 768), L16("s16", 0, C)
 
     def parents(k):
-        cp(R("LP%d" % k, 0, 768, 1, W("lU%d" % k)), R("iotaF", 0, C))
-        scan(R("lpS", 0, C), R("d16n", 0, C), R("LP%d" % k, 0, C))
-        ts(W("lpU"), L16("lpS"), CORR, OP.subtract)
-        tt(W("PK", 24), L16("lpS"), W("n16"), OP.subtract)
+        cp(R("LP%d" % k, 0, 768, 1, W("lU%d" % k)), R("cval", 0, C))
+        scan(R("lpS", 0, C), R("d16h", 0, C), R("LP%d" % k, 0, C))
+        ts(W("lpU"), L16("lpS"), LPC, OP.subtract)
 
-    def columns():
-        ts(W("lcW"), L16("s16l"), TH16, OP.is_ge, 384.0, OP.mult)
-        tt(W("lcX"), L16("s16l"), W("lcW"), OP.subtract)
-        ts(W("lcU"), W("lcX"), CORR, OP.subtract)
+    def columns(a):
+        n = 36 - (768 - a) // 16
+        s = L16("s16", a, 768)
+        ts(R("colW", n, 36), s, TH16, OP.is_ge, 384.0, OP.mult)
+        tt(R("colX", n, 36), s, R("colW", n, 36), OP.subtract)
+        ts(R("colU", n, 36), R("colX", n, 36), CORR, OP.subtract)
 
-    def structure():
-        offsets_d("KD", L16("s16l"))
-        scan(R("aS", 0, C), R("d16h", 0, C), R("aF", 0, C))
-        tt(W("RL"), L16("s16r"), L16("s16l"), OP.subtract)
-        tt(W("A"), L16("aS"), L16("s16l"), OP.subtract)
+    def ways(d, e, l, c):
+        tt(slot(d, 1), l, c, OP.subtract)
+        act(slot(e, 1, 4, 24), slot(d, 1), ACT.Copy)
+        act(slot(d, 1, 4, 24), slot(d, 1), ACT.Copy, -1.0, -384.0)
 
-    def offsets_d(n, l): tt(W(n), l, W("n16"), OP.subtract)
-
-    def offsets_e(n):
-        act(W(n, 24), W(n), ACT.Copy)
-        act(W(n, 48), W(n), ACT.Copy, -1.0, -384.0)
-
-    cp(W("lU0"), W("ltI")); ts(L16("s16l"), W("ltI"), CORR, OP.add)
-    quant("q_u", 0, 128, "ut", 0)
-    run("s", lambda e: e.activation(T.uls[:, 0:512], T.q_us[:, 0:128].indirect(ap(R("uU", 0, 32))), ACT.Copy), [R("q_u", 0, 128), R("uU", 0, 32)], [R("uls", 0, 512)])
-    run("v", lambda e: e.tensor_copy(T.ul[:, 0:512].bitcast(dt.uint32), T.q_u[:, 0:128].bitcast(dt.uint32).indirect(ap(R("uU", 0, 32)))), [R("q_u", 0, 128), R("uU", 0, 32)], [R("ul", 0, 512)])
-    cp(W("rU"), W("rtI")); ts(L16("s16r"), W("rtI"), CORR, OP.add)
-    act(R("LR0", 0, C), R("iotaF", 0, 768, 1, W("lU0")), ACT.Copy)
-    act(R("LR0", C, 768), R("iotaF", 0, 768, 1, W("rU")), ACT.Copy)
-    act(R("d16h", 0, C), R("d16n", 0, C), ACT.Copy)
-    quant("q_x", 0, C, "X0", 0)
+    cp(W("lU0"), W("ltI"))
+    ts(SL, W("ltI"), CORR, OP.add)
+    columns(C)
     parents(0)
-    columns()
-    fill(R("PK", 0, 24), 384.0)
+    act(R("LR0", C, 768), R("iotaF", 0, 768, 1, W("lU0")), ACT.Copy)
 
     bank = lambda k, n: R("psS", 512 * k, 512 * k + n)
 
@@ -319,184 +297,186 @@ def rank_program(g, core, T, topo):
         for k in range(4): mm(bank(k, b - a), "ul", 128 * k, "q_x", a, b - a)
 
     def sign1(a, b):
-        act(R("sA1", a, b), bank(0, b - a), ACT.Sign)
-        if b == HALF: ts(R("TB1", a, b), bank(1, b - a), 0.0, OP.is_le, 0.25, OP.mult)
-        else:
-            act(R("tb", a, b), bank(1, b - a), ACT.Sign, -1.0, TINY)
-            act(R("TB1", a, b), R("tb", a, b), ACT.Copy, 0.125, 0.125)
+        act(R("sA1", 16 + a, 16 + b), bank(0, b - a), ACT.Sign)
+        ts(R("TB1", a, b), bank(1, b - a), 0.0, OP.is_le, 0.25, OP.mult)
 
-    def sign2(a, b):
-        act(R("sA", a, b), bank(2, b - a), ACT.Sign)
-        act(R("TB2", a, b), bank(3, b - a), ACT.Sign, -1.0, TINY)
-        gcopy(R("TB2", C + a, C + b), R("TB2", a, b), b - a)
-        act(R("sA2", a, b), R("sA", a, b), ACT.Copy, 4.0)
+    def sign2(a, b): act(R("sA2", a, b), bank(2, b - a), ACT.Sign)
 
-    def roots2(a, b): tt(R("vm", a, b), bank(2, b - a), R("tiny", a, b), OP.min)
-    def value2(a, b): act(R("val", a, b), R("vm", a, b), ACT.Relu, UP)
+    def turns2(a, b):
+        act(R("oT", 1536 + a, 1536 + b), bank(3, b - a), ACT.Sign, -1.0, TINY)
+        gcopy(R("oT", 1920 + a, 1920 + b), R("oT", 1536 + a, 1536 + b))
 
-    def roots(kd, gsc, m, tm, bs):
-        tt(W(m, 24), L16(gsc), W("T1"), OP.is_lt)
-        tt(W(m, 48), L16(gsc), W("T2"), OP.is_lt)
-        tt(R(tm, 0, 72), R(m, 0, 72), R(kd, 0, 72), OP.mult)
-        tt(R(bs, 0, 48), R(tm, 0, 48), R("base", 0, 48), OP.add)
-        tt(W(bs, 24), W(bs, 24), W(tm, 48), OP.add)
+    def halves(a):
+        dma("g", T.XYh[:, a:a + 768], T.XYh[:, 1536 + a:2304 + a], [R("XYh", 1536 + a, 2304 + a), R("XYh", a, a + 768)], [R("XYh", a, a + 768)], 3.0, 1.0, accum_op=OP.add)
 
     for k in range(3):
         p = T.cores[rank ^ STEP[k]]
         last = k == 2
         X, XN = "X%d" % (k % 2), "X%d" % (1 - k % 2)
-        LRk, LMk, LRn, lU = "LR%d" % k, "LM%d" % k, "LR%d" % (k + 1), "lU%d" % k
+        LRk, LRn, lU = "LR%d" % k, "LR%d" % (k + 1), "lU%d" % k
         a0, b0 = (0, C) if k == 0 else (0, HALF)
         scores(a0, b0)
-        if k: structure()
         sign1(a0, b0)
-        tt(R("oA", 0, C), R("TB1", 0, C, 1, W("lcU")), R("sA1", 0, C), OP.add)
-        act(R("hpF", 0, C), R("sA1", 0, 768, 1, W("lpU")), ACT.Copy, -1.0)
-        act(R("GA", 0, C), R("oA", 0, 768, 1, W(lU)), ACT.Copy)
-        if k == 0: act(R("aF", 0, C), R("LR0", 0, 768, 1, W("lU0")), ACT.Copy)
-        sign2(a0, b0)
+        tt(R("oT", 0, C), R("TB1", 0, C, 1, R("colU", 12, 36)), R("sA1", 16, 16 + C), OP.add)
         if k == 0:
-            offsets_d("KD", L16("s16l"))
-            tt(W("RL"), L16("s16r"), L16("s16l"), OP.subtract)
-        offsets_e("KD")
-        if k == 0:
-            act(R("d16c", 0, C), R("d16n", 0, C), ACT.Copy, PAR)
-            act(R("d4h", 0, C), R("d4n", 0, C), ACT.Copy)
-        scan(R("oS", 0, C), R("d16b", 0, C), R("oA", 0, C))
+            act(R("aF", 0, C), R(LRk, C, 768, 1, R("colU", 12, 36)), ACT.Copy)
+            sign2(a0, b0)
+        act(R("hpF", 0, C), R("sA1", 0, 16 + C, 1, W("lpU")), ACT.Copy, -1.0)
+        if k == 0: turns2(a0, b0)
+        act(R("GA", 0, C), R("oT", 0, 768, 1, W(lU)), ACT.Identity, -1.0, GB0)
+        if k:
+            sign2(a0, b0)
+            act(R("aF", 0, C), R(LRk, C, 768, 1, R("colU", 12, 36)), ACT.Copy)
         scan(R("oS", C, 768), R("d16b", 0, C), R("hpF", 0, C))
-        ts(W("hh"), L16("oS"), THH, OP.is_gt, 100.0, OP.mult)
-        ts(R("ET", 0, 48), L16("oS", 768), TE, OP.is_lt)
-        ts(W("HP"), L16("oS"), TT, OP.is_lt)
-        ts(W("T2"), W("hh"), TTM, OP.add)
-        tt(W("AT", 24), W("ET"), W("ET", 24), OP.mult)
-        tt(W("AT"), W("HP"), W("ET", 24), OP.mult)
-        act(W("T1"), W("hh"), ACT.Identity, 1.0, TEM)
+        scan(R("oS", 0, C), R("d16b", 0, C), R("oT", 0, C))
+        scan(R("s2S", 0, C), R("d16b", 0, C), R("sA2", 0, C))
+        tt(W("x0"), L16("oS"), L16("oS", C, 768), OP.add)
         scan(R("gS", 0, C), R("d16b", 0, C), R("GA", 0, C))
-        tt(W("bl"), W("AT"), W("RL"), OP.mult)
-        tt(W("bl2"), W("bl"), L16("s16l"), OP.add)
+        act(W("T0"), L16("oS"), ACT.Relu, -100.0, KT)
+        act(W("ct"), W("x0"), ACT.Relu, -4.0, X4)
+        act(slot("EA", 3, 5), L16("s2S"), ACT.Relu, -768.0, KS)
+        scan(R("aS", 0, C), R("d16h", 0, C), R("aF", 0, C))
+        tt(slot("DA", 1, 5), L16("aS"), SL, OP.subtract)
         if k == 0:
-            scan(R("aS", 0, C), R("d16h", 0, C), R("aF", 0, C))
-            tt(W("A"), L16("aS"), L16("s16l"), OP.subtract)
-        tt(W("M"), L16("gS"), W("T2"), OP.is_lt)
-        tt(W("mA"), W("M"), W("A"), OP.mult)
-        tt(W("l2W"), W("mA"), W("bl2"), OP.add)
-        ts(W("l2U"), W("l2W"), CORR, OP.subtract)
-        if k == 0:
-            ts(R("XYh", 0, 1536), R("X0", 0, 1536), 0.5, OP.mult)
-            ts(R("XYh", 2688, 3072), R("LV", 1152, 1536), 0.5, OP.mult)
-        tt(R("oB", 0, C), R("TB2", 0, 768, 1, W("l2U")), R("sA2", 0, C), OP.add)
-        roots2(a0, b0)
-        if k == 0:
-            iota(R("imod", 0, 768), [[0, 2], [1, 384]], 0, 0, True)
-            for i in (1, 2):
-                iota(R("LP%d" % i, 0, C), [[0, C]], 400, 0, True)
-                iota(R("CP%d" % i, 0, C), [[0, C]], 0, 0, True)
-        if k:
-            for b in range(4):
-                act(R("XYh", 1536 + b, 2304, 4), R("psH", 512 * b, 512 * b + HALF), ACT.Copy, 0.5)
-        act(R("GB", 0, C), R("oB", 0, 768, 1, W("l2U")), ACT.Copy)
-        value2(a0, b0)
-        tt(R("AP", 0, 48), R("AT", 0, 48), R("PK", 0, 48), OP.mult)
-        roots("KD", "gS", "M", "TM", "bs")
-        tt(R("sg1", 0, 48), R("AP", 0, 48), R("bs", 0, 48), OP.add)
-        cp(R("sg1U", 0, 48), R("sg1", 0, 48))
-        scan(R("o2S", 0, C), R("d16b", 0, C), R("oB", 0, C))
-        act(W("s1"), L16("o2S"), ACT.Sign, 1.0, NH2)
-        act(W("T2"), W("s1"), ACT.Identity, 50.0, S2M)
-        act(W("T1"), W("s1"), ACT.Identity, 50.0, E2M)
-        act(W("sE"), L16("o2S"), ACT.Sign, -1.0, S2)
-        act(W("sE", 24), L16("o2S"), ACT.Sign, -1.0, E2)
-        act(W("fl2"), W("sE"), ACT.Relu, 384.0)
-        act(W("fl2", 24), W("sE", 24), ACT.Relu, 1.0 / PAR)
-        act(R(LMk, 0, C), R(LRk, 0, 768, 1, W("sg1U")), ACT.Copy)
-        act(R(LMk, C, 768), R(LRk, 0, 768, 1, W("sg1U", 24)), ACT.Copy)
-        cp(R("CP%d" % k, 0, 768, 1, W("l2U")), R("val", 0, C))
-        offsets_d("KD2", W("l2W"))
-        offsets_e("KD2")
-        if k:
-            for a in (768, 0): act(R("XYh", a, a + 768), R(X, a, a + 768), ACT.Copy, 0.5)
-        else:
-            act(R("XYh", 1536, 2688), R("LV", 0, 1152), ACT.Copy, 0.5)
+            cp(W("rU"), W("rtI")); ts(SR, W("rtI"), CORR, OP.add)
+        tt(W("RL"), SR, SL, OP.subtract)
+        ts(slot("EA", 2, 5), SL, CORR, OP.subtract)
+        tt(slot("EA", 0, 5), L16("gS"), W("T0"), OP.is_gt)
+        tt(slot("EA", 1, 5), W("ct"), W("RL"), OP.mult)
+        ts(slot("EA", 4, 5), L16("s2S"), KAP, OP.is_equal, 768.0, OP.mult)
+        if k: turns2(a0, b0)
+        chain("OA", "DA", "EA", 120)
+        cp(W("iN"), slot("OA", 3, 5))
+        act(R("oT", 0, C), R("oT", 768, 2304, 1, W("iN")), ACT.Copy)
+        cp(W("iP"), slot("OA", 4, 5))
+        act(R("GB", 0, C), R("oT", 0, 1536, 1, W("iP")), ACT.Copy)
+        ways("DB", "EB", SL, W("n16"))
+        tt(W("PK"), L16("lpS"), W("n2"), OP.subtract)
+        act(slot("EB", 0), slot("EA", 0, 5), ACT.Copy)
+        act(slot("EB", 0, 4, 24), slot("EA", 0, 5), ACT.Copy)
+        act(slot("EB", 1), W("x0"), ACT.Relu, -1536.0, X384)
+        ts(W("ca"), W("x0"), XA, OP.is_lt)
+        tt(slot("EB", 2, 4, 24), W("ca"), W("PK"), OP.mult)
+        tt(slot("DB", 2, 4, 24), L16("gS"), W("T0"), OP.is_ge)
+        chain("OB", "DB", "EB", 192)
+        cp(R("sg1U", 0, 48), slot("OB", 3, 4, 0, 48))
+        cp(R("CP%d" % k, 0, 1536, 1, W("iP")), R("cval", 0, C))
+        if k == 0: act(R("LR0", 768, 1152), R("iotaF", 0, 768, 1, W("rU")), ACT.Copy)
+        act(R("LM", C, 768), R(LRk, C, 1152, 1, W("sg1U", 24)), ACT.Copy)
+        act(R("LM", 0, C), R(LRk, C, 1152, 1, W("sg1U")), ACT.Copy)
+        scan(R("o2S", 0, C), R("d16b", 0, C), R("oT", 0, C))
+        scan(R("cS", 0, C), R("d16h", 0, C), R("CP%d" % k, 0, C))
+        ts(W("Tc"), L16("o2S"), KAP, OP.is_equal, 4096.0, OP.mult)
+        ts(W("u1"), L16("cS"), UC, OP.subtract)
         scan(R("g2S", 0, C), R("d16b", 0, C), R("GB", 0, C))
-        tt(W("M2"), L16("g2S"), W("T2"), OP.is_lt)
-        roots("KD2", "g2S", "M2", "TM2", "bs2")
-        scan(R("cS", 0, C), R("d16c", 0, C), R("CP%d" % k, 0, C))
-        ts(W("hp2"), L16("cS"), CORRC, OP.is_gt)
-        tt(W("PK2"), L16("cS"), W("n1"), OP.subtract)
-        tt(W("AP2"), W("fl2"), W("hp2"), OP.mult)
-        tt(W("AT2"), W("fl2", 24), W("hp2"), OP.mult)
-        tt(W("AP2", 24), W("AT2"), W("PK2"), OP.mult)
-        tt(R("sg", 0, 48), R("AP2", 0, 48), R("bs2", 0, 48), OP.add)
-        cp(R("sgU", 0, 48), R("sg", 0, 48))
-        cp(R("R3h", 0, C), R(LMk, 0, 768, 1, W("sgU", 24)))
-        act(R("L3h", 0, C), R(LMk, 0, 768, 1, W("sgU")), ACT.Copy)
+        tt(W("ca1"), W("u1"), W("Tc"), OP.is_gt)
+        tt(W("PK1"), L16("cS"), W("n2"), OP.subtract)
+        ts(W("N2"), L16("o2S"), KLO, OP.is_lt, 384.0, OP.mult)
+        tt(slot("EC", 2, 4, 24), W("ca1"), W("PK1"), OP.mult)
+        tt(slot("EC", 1), W("u1"), W("N2"), OP.min)
+        if OPT["sflags"]:
+            act(slot("EC", 0), L16("g2S"), ACT.Relu, -1.0, KAP)
+            act(slot("EC", 0, 4, 24), L16("g2S"), ACT.Relu, -1.0, KAP)
+            act(slot("DC", 2, 4, 24), L16("g2S"), ACT.Abs, 1.0, NKAP)
+        else:
+            ts(slot("EC", 0), L16("g2S"), KLO, OP.is_lt)
+            ts(slot("EC", 0, 4, 24), L16("g2S"), KLO, OP.is_lt)
+            ts(slot("DC", 2, 4, 24), L16("g2S"), KAP, OP.not_equal)
+        ways("DC", "EC", slot("OA", 2, 5), W("base"))
+        chain("OC", "DC", "EC", 192)
+        cp(R("sgU", 0, 48), slot("OC", 3, 4, 0, 48))
+        cp(R("R3h", 0, C), R("LM", 0, 768, 1, W("sgU", 24)))
+        act(R("L3h", 0, C), R("LM", 0, 768, 1, W("sgU")), ACT.Copy)
+        if k == 0:
+            ts(R("p3", 0, 1), R("pI", 0, 1), 3, OP.bitwise_and)
+            cp(I3, R("p3", 0, 1))
+            ts(R("v4m", 0, 16), R("v4", 0, 16), 15, OP.bitwise_and)
+            ts(R("u16", 0, 16), R("v4m", 0, 16), 4.0, OP.is_lt, RESET, OP.mult)
+            ts(R("u16", 16, 32), R("v4m", 0, 16), 12.0, OP.is_ge, LIFT, OP.mult)
+            tt(R("d4h", 0, 16), R("u16", 0, 16), R("u16", 16, 32), OP.add)
+            ts(C12, I15, 12.0, OP.is_lt, LIFT, OP.mult)
+            ts(ADD4, C12, -4.0, OP.mult, I3, OP.add)
+            act(TH4, C12, ACT.Copy, 1.0, 384.0)
+            widen("d4h")
+            for a in range(0, 1536, 256): act(R("XYh", 1536 + a, 1792 + a), R("LV", a, a + 256), ACT.Copy, 0.5)
+            for a in range(0, 1536, 256): ts(R("XYh", a, a + 256), R("X0", a, a + 256), 0.5, OP.mult)
         scan(R("sR4", 0, C), R("d4h", 0, C), R("R3h", 0, C))
         ts(R("oR", 0, 96), R("sR4", 3, C, 4), 4.0, OP.mult, ADD4, OP.add)
-        PIECES = ((0, 64), (64, 128), (128, 256), (256, 384))
+        cuts = OPT["pieces"]
+        PIECES = list(zip(cuts, cuts[1:]))
         for a, b in PIECES:
             act(R("Rg", 4 * a, 4 * b), R("XYh", 0, 3072, 1, R("oR", a // 4, b // 4)), ACT.Copy)
-        gcopy(R("LD", 0, C), R("L3h", 0, C), C)
-        scan(R("s16r", 0, C), R("d16h", 0, C), R("R3h", 0, C))
+        scan(R("s16", 0, HALF), R("d16h", 0, HALF), R("R3h", 0, HALF))
         scan(R("sL4", 0, C), R("d4h", 0, C), R("L3h", 0, C))
-        ts(R("rU%d" % k, 0, 24), L16("s16r"), CORR, OP.subtract)
+        ts(R("rU%d" % k, 0, 12), L16("s16", 0, HALF), CORR, OP.subtract)
         ts(R("oL", 0, 96), R("sL4", 3, C, 4), 4.0, OP.mult, ADD4, OP.add)
-        remote(p, T["rin%d" % k][:, :], ap(R("rU%d" % k, 0, 12)), [R("rU%d" % k, 0, 12)], "ar%d" % k, R("rin%d" % k, 0, 12), 2.2)
-        gcopy(R("LD", C, 768), R("L3h", 0, C), C)
-        scan(R("s16l", 0, C), R("d16h", 0, C), R("L3h", 0, C))
-        ts(W("lU%d" % (k + 1)), L16("s16l"), CORR, OP.subtract)
-        remote(p, T["lin%d" % k][:, :], ap(W("lU%d" % (k + 1))), [W("lU%d" % (k + 1))], "al%d" % k, W("lin%d" % k), 2.2)
+        gcopy(R(LRn, C, 768), R("L3h", 0, C))
+        remote(p, T["rin%d" % k][:, :], ap(R("rU%d" % k, 0, 12)), [R("rU%d" % k, 0, 12)], "ar%d" % k, R("rin%d" % k, 0, 12), OPT["list"] + (1.5 if k == 0 else 0), 0)
+        scan(R("s16", C, 768), R("d16h", 0, C), R("L3h", 0, C))
+        ts(W("lU%d" % (k + 1)), SL, CORR, OP.subtract)
+        remote(p, T["lin%d" % k][:, :], ap(W("lU%d" % (k + 1))), [W("lU%d" % (k + 1))], "al%d" % k, W("lin%d" % k), OPT["list"] + (1.0 if k == 0 else 0), 1)
+        gcopy(R(LRn, 0, C), R("L3h", 0, C))
         for c in range(3):
             for a, b in PIECES:
-                if a // 128 == c: tt(R("Z", 4 * a, 4 * b), R("XYh", 0, 3072, 1, R("oL", a // 4, b // 4)), R("Rg", 4 * a, 4 * b), OP.add)
+                if (b - 1) // 128 == c: tt(R("Z", 4 * a, 4 * b), R("XYh", 0, 3072, 1, R("oL", a // 4, b // 4)), R("Rg", 4 * a, 4 * b), OP.add)
             quant("q_z", 128 * c, 128 * c + 128, "Z", 128 * c)
+        for c in range(3):
             for b in range(4):
-                o = R("psH", 512 * b, 512 * b + 128)
+                o = R("psS" if c == 1 else "psH", 512 * b, 512 * b + 128)
+                h = R("H", 512 * c + b, 512 * c + 512, 4)
                 mm(o, "q_w", 128 * b, "q_z", 128 * c, 128)
-                act(R("H", 512 * c + b, 512 * c + 512, 4), o, ACT.Copy, 0.03125)
-        cp(R("mF", 0, HALF), R("LD", 0, 768, 1, R("rin%d" % k, 0, 12)))
+                if c == 2 and b % 2 == 0 and b < 2 * OPT["hv"]: ts(h, o, 0.03125, OP.mult)
+                else: act(h, o, ACT.Copy, 0.03125)
+        pick(OPT["mfs"], R("mF", 0, HALF), R(LRn, 0, 768, 1, R("rin%d" % k, 0, 12)))
         scan(R("mS", 0, HALF), R("d4h", 0, HALF), R("mF", 0, HALF))
         m4 = R("mS", 3, HALF, 4)
         ts(R("mm", 0, 48), m4, TH4, OP.is_ge, -1536.0, OP.mult)
         act(R("mo", 0, 48), m4, ACT.Identity, 4.0, ADD4)
         tt(R("ms", 0, 48), R("mm", 0, 48), R("mo", 0, 48), OP.add)
         cp(R("mfU", 0, 48), R("ms", 0, 48))
-        cp(R("F", 0, 384), R("H", 0, 1536, 1, R("mfU", 0, 24)))
-        act(R("F", 384, 768), R("H", 0, 1536, 1, R("mfU", 24, 48)), ACT.Copy)
+        fs = OPT["fsplit"]
+        cp(R("F", 0, 16 * fs), R("H", 0, 1536, 1, R("mfU", 0, fs)))
+        act(R("F", 16 * fs, 768), R("H", 0, 1536, 1, R("mfU", fs, 48)), ACT.Copy)
         quant("fq%d" % k, 0, HALF, "F", 0)
-        remote(p, T["cin%d" % k][:, 0:HALF].bitcast(dt.uint8), T["fq%d" % k][:, 0:HALF].bitcast(dt.uint8), [R("fq%d" % k, 0, HALF)], "ac%d" % k, R("cin%d" % k, 0, HALF), 3.7)
-        remote(p, T["sin%d" % k][:, 0:HALF], T["fs%d" % k][:, 0:HALF], [R("fq%d" % k, 0, HALF)], "as%d" % k, R("sin%d" % k, 0, HALF), 2.7)
+        remote(p, T["cin%d" % k][:, 0:HALF].bitcast(dt.uint8), T["fq%d" % k][:, 0:HALF].bitcast(dt.uint8), [R("fq%d" % k, 0, HALF)], "ac%d" % k, R("cin%d" % k, 0, HALF), OPT["far"])
+        remote(p, T["sin%d" % k][:, 0:HALF], T["fs%d" % k][:, 0:HALF], [R("fq%d" % k, 0, HALF)], "as%d" % k, R("sin%d" % k, 0, HALF), OPT["far"])
+        gcopy(R(LRn, 768, 1152), R("R3h", 0, C))
+        if k == 0:
+            iota(R("imod", 0, 768), [[0, 2], [1, 384]], 0, 0, True)
+            run("g", lambda e: e.affine_select(T.E[:, 0:528], T.ones[:, 0:528], [[1, 528]], OP.is_equal, 0.0, -3, -4), [R("ones", 0, 528)], [R("E", 0, 528)], 1.2)
+        if not last:
+            gfill(R("LP%d" % (k + 1), 0, C), NONE0)
+            gfill(R("CP%d" % (k + 1), 0, C), NONE1)
+        scan(R("s16", HALF, C), R("d16h", 0, HALF), R("R3h", HALF, C))
+        columns(HALF)
         act(R("LPp", 0, C), R("imod", 0, 768, 1, W("lin%d" % k)), ACT.Copy)
-        act(R("LPp", C, 768), R("imod", 0, 768, 1, W("lin%d" % k)), ACT.Copy)
-        act(R("nF", 0, HALF), R("LPp", 0, 768, 1, R("rU%d" % k, 12, 24)), ACT.Copy)
-        act(R(LRn, C, 768), R(LMk, 0, 768, 1, W("sgU", 24)), ACT.Copy)
-        act(R(LRn, 0, C), R("L3h", 0, C), ACT.Copy)
-        if last: dma("y", T.gr[:, :], T[LRn][0:128:16, :], [R(LRn, 0, 768)], [])
-        if not last: parents(k + 1)
+        act(R("nF", 0, HALF), R("LPp", 0, C, 1, R("colU", 0, 12)), ACT.Copy)
+        if last: dma("y", T.gr[:, :], T[LRn][0:128:16, C:], [R(LRn, C, 1152)], [])
+        if not last and OPT["lp"] == 0: parents(k + 1)
         scan(R("mnS", 0, HALF), R("d4h", 0, HALF), R("nF", 0, HALF))
         ts(R("mnU", 0, 48), R("mnS", 3, HALF, 4), 4.0, OP.mult, ADD4, OP.add)
         tt(R(XN, 768, 1536), R("H", 0, 1536, 1, R("mnU", 0, 48)), R(X, 768, 1536), OP.add)
         quant("q_x", HALF, C, XN, HALF)
+        if not last and OPT["lp"] == 1: parents(k + 1)
         if k == 0:
-            quant("q_e", 0, 512, "E", 0)
-            quant("q_v", 0, 128, "vt", 0)
+            for b in range(4): quant("q_e", 128 * b, 128 * b + 128, "E", 0, 3 - b)
+        if last: quant("q_v", 0, 128, "vt", 0)
 
         def finish(a):
             o = bank(a > 0, HALF)
             mm(o, "q_v", 0, "q_x", a, HALF)
             act(R("yS", a, a + HALF), o, ACT.Copy)
+            dma("y" if a else "s", T.y[:, a:a + HALF], T.yS[:, a:a + HALF], [R("yS", a, a + HALF)], [])
             dma("y", T.oc[:, 4 * a:4 * a + 4 * HALF], T.q_x[:, a:a + HALF].bitcast(dt.uint8), [R("q_x", a, a + HALF)], [])
             for i in range(4):
                 dma("y", T.osc[4 * i:4 * i + 4, a:a + HALF], T.q_xs[32 * i:32 * i + 4, a:a + HALF], [R("q_x", a, a + HALF)], [])
-            dma("y" if a else "s", T.y[:, a:a + HALF], T.yS[:, a:a + HALF], [R("yS", a, a + HALF)], [])
         if not last:
-            act(R("XYh", 2304, 3072), R("H", 0, 1536, 1, R("mnU", 0, 48)), ACT.Copy, 0.5)
             scores(HALF, C)
-            columns()
-            roots2(HALF, C)
             sign1(HALF, C)
             sign2(HALF, C)
-            value2(HALF, C)
-            act(R("aF", 0, C), R(LRn, 0, 768, 1, W("lU%d" % (k + 1))), ACT.Copy)
+            turns2(HALF, C)
+            act(R("XYh", 2304, 3072), R("H", 0, 1536, 1, R("mnU", 0, 48)), ACT.Copy, 0.5)
+            halves(768)
         else:
             finish(HALF)
         for b in range(4):
@@ -505,4 +485,7 @@ def rank_program(g, core, T, topo):
             tt(R(XN, b, 768, 4), R(X, b, 768, 4), R("psH", 512 * b, 512 * b + HALF), OP.add)
         quant("q_x", 0, HALF, XN, 0)
         if last: finish(0)
+        else:
+            for b in range(4): act(R("XYh", 1536 + b, 2304, 4), R("psH", 512 * b, 512 * b + HALF), ACT.Copy, 0.5)
+            halves(0)
     emit()

@@ -5,8 +5,9 @@ OP, ACT = AluOpType, ActivationFunctionType
 RESET, LIFT = -4096.0, 1024.0
 TINY = 2.0 ** -101
 MID, NONE0, NONE1 = 192.0, -208.0, -576.0
-CY = 0.00095
-OPT = {"wake": 0.08, "hv": 2, "fsplit": 24, "sflags": 0, "mfs": 1, "far": 3.4, "list": 1.8, "pe": 0.00125, "pieces": (0, 64, 128, 256, 384), "lp": 0, "room": 0.2}
+CY = 0.00085
+OPT = {"wake": 0.14, "room": 0.15, "list": 2.1, "first": 1.2, "far": 2.0, "on": 0.5, "pe": 0.00125,
+       "pieces": (0, 64, 128, 192, 256, 384), "hv": (8, 9, 10, 11), "yS": 1024, "lpn": 24, "two": 1, "fsplit": 24}
 
 SCRATCH = {}
 PLACE = {}
@@ -23,7 +24,7 @@ def _share(buf, t, items):
 
 
 for _n, _w in (("X0", 1536), ("X1", 1536), ("LV", 1536), ("XYh", 3072), ("H", 1536), ("Z", 1536), ("Rg", 1536), ("F", 768),
-               ("ut", 512), ("vt", 512), ("E", 528), ("ones", 528), ("sA1", 16 + C), ("sA2", C), ("TB1", C),
+               ("ut", 512), ("vt", 512), ("E", 528), ("ones", 528), ("sA1", 16 + C), ("sA2", C), ("TB1", C), ("tb", HALF),
                ("oT", 2304), ("hpF", C), ("GA", C), ("GB", C), ("oS", 768), ("gS", C), ("s2S", C), ("o2S", C), ("g2S", C),
                ("d16b", C), ("cval", C)):
     _sb(_n, _w, "bfloat16")
@@ -32,16 +33,18 @@ for _n, _w in (("iotaF", 768), ("imod", 768), ("LPp", C), ("LM", 768), ("yS", C)
 for _n, _w in (("mF", HALF), ("mS", HALF), ("nF", HALF), ("mnS", HALF), ("d4h", C), ("d16h", C), ("L3h", C), ("R3h", C),
                ("sR4", C), ("sL4", C), ("s16", 768), ("aF", C), ("aS", C), ("lpS", C), ("cS", C)):
     _sb(_n, _w, "float16")
-_share("wf", "float32", (("cst", 32), ("base", 48), ("n16", 24), ("n2", 24), ("t16", 32), ("u16", 32), ("colW", 40), ("colX", 40), ("RL", 24), ("PK", 24), ("x0", 24),
+_share("wf", "float32", (("cst", 32), ("base", 48), ("n16", 24), ("n2", 24), ("t16", 32), ("u16", 32), ("colW", 48), ("colX", 48), ("RL", 24), ("PK", 24), ("x0", 24),
                          ("ct", 24), ("ca", 24), ("T0", 24), ("N2", 24), ("Tc", 24), ("u1", 24), ("ca1", 24), ("PK1", 24), ("mm", 48), ("mo", 48), ("ms", 48)))
 _share("wh", "float16", (("DA", 120), ("DB", 192), ("DC", 192), ("EB", 192), ("EC", 192), ("EA", 120), ("OA", 120), ("OB", 192), ("OC", 192)))
 _share("wi", "int32", (("pI", 1), ("p15", 1), ("p3", 1), ("v16", 16), ("v16m", 16), ("v4", 16), ("v4m", 16), ("nI", 24), ("uI", 32)))
-_share("wu", "uint16", [("rU%d" % _k, 12) for _k in range(3)] + [("lU%d" % _k, 24) for _k in range(4)] +
-       [("rU", 24), ("colU", 40), ("lpU", 24), ("iP", 24), ("iN", 24), ("sgU", 48), ("sg1U", 48), ("oR", 96), ("oL", 96), ("mfU", 48), ("mnU", 48), ("uU", 32)])
+_share("wu", "uint16", [("rU%d" % _k, 36) for _k in range(3)] +
+       [("lU0", 24), ("rU", 24), ("colU", 40), ("lpU", 24), ("iP", 24), ("iN", 24), ("sgU", 48), ("sg1U", 48), ("oR", 96), ("oL", 96), ("mfU", 48), ("mnU", 48), ("uU", 32)])
 _sb("ltI", 24, "int32"); _sb("rtI", 24, "int32")
 for _k in range(3):
+    PLACE["lU%d" % (_k + 1)] = ("wu", PLACE["rU%d" % _k][1] + 12)
+    PLACE["lin%d" % _k] = ("rin%d" % _k, 12)
+    _sb("rin%d" % _k, 36, "uint16")
     _sb("LP%d" % _k, 768, "bfloat16"); _sb("CP%d" % _k, 1536, "bfloat16")
-    _sb("rin%d" % _k, 12, "uint16"); _sb("lin%d" % _k, 24, "uint16")
     _sb("fq%d" % _k, HALF, "float8_e4m3fn_x4"); _sb("fs%d" % _k, HALF, "uint8")
     _sb("cin%d" % _k, HALF, "float8_e4m3fn_x4"); _sb("sin%d" % _k, HALF, "uint8")
 for _k in range(4): _sb("LR%d" % _k, 3 * C, "float32")
@@ -180,7 +183,6 @@ def rank_program(g, core, T, topo):
         kw = {n: x for n, x, d in (("scale", scale, 1.0), ("bias", bias, 0.0)) if x != d}
         kv = {n: ap(x) if isinstance(x, tuple) else x for n, x in kw.items()}
         run("s", lambda e: e.activation(ap(o), ap(a), f, **kv), [a] + [x for x in kw.values() if isinstance(x, tuple)], [o], picked(o, a) if a[4] else plain(width(o)))
-    def pick(on_scalar, o, a): act(o, a, ACT.Copy) if on_scalar else cp(o, a)
     def sfill(o, c): act(o, R("ones", 0, width(o)), ACT.Copy, c)
     def quant(q, a, b, tile, ta, shift=0):
         i = R(tile, 4 * ta + shift, 4 * (ta + b - a) + shift)
@@ -195,7 +197,7 @@ def rank_program(g, core, T, topo):
     def gfill(o, c): iota(o, [[0, width(o)]], int(c), 0, True)
     def gcopy(o, a):
         run("g", lambda e: e.affine_select(ap(o), ap(a), [[0, width(o)]], OP.is_ge, 0.0, 0, 0), [a], [o], 0.2 + width(o) * 2 * CY)
-    I15, I3, CORR, C12, ADD4, TH4, TH16, KAP, NKAP, KLO, XA, GB0, KS, LPC, UC, KT, X4, X384 = [R("cst", i, i + 1) for i in range(18)]
+    I15, I3, CORR, C12, ADD4, TH4, TH16, KAP, NKAP, NCORR, XA, GB0, KS, LPC, UC, KT, X4, X384, K384 = [R("cst", i, i + 1) for i in range(19)]
 
     def lane(k, a, b): act(k, CORR, ACT.Copy, a, b)
 
@@ -218,14 +220,34 @@ def rank_program(g, core, T, topo):
     load("y", "q_ws", T.ws[:, :], 0, 512, None, [R("X0", 0, 1536)], 3.0)
     load("y", "vt", T.v[:, :], 0, 512, None, [R("X0", 0, 1536)], 3.0)
 
+    SL, SR = L16("s16", C, 768), L16("s16", 0, C)
+
+    def columns(s, a, b, o):
+        ts(R("colW", a, b), s, TH16, OP.is_ge, 384.0, OP.mult)
+        tt(R("colX", a, b), s, R("colW", a, b), OP.subtract)
+        ts(o, R("colX", a, b), CORR, OP.subtract)
+    iota(R("pI", 0, 1), [[1, 1]], 0, 1)
     iota(R("uI", 0, 32), [[1, 4], [16, 8]], 0, 0)
+    ts(R("p15", 0, 1), R("pI", 0, 1), 15, OP.bitwise_and)
+    cp(I15, R("p15", 0, 1))
+    ts(CORR, I15, 15.0, OP.is_lt, LIFT, OP.mult)
+    lane(TH16, 1.0, 384.0)
+    cp(W("lU0"), W("ltI"))
+    ts(SL, W("ltI"), CORR, OP.add)
+    columns(SL, 24, 48, R("colU", 12, 36))
     cp(R("uU", 0, 32), R("uI", 0, 32))
     quant("q_u", 0, 128, "ut", 0)
     for a in (0, 256):
         o = R("uU", a // 16, a // 16 + 16)
-        run("s", lambda e, a=a, o=o: e.activation(T.uls[:, a:a + 256], T.q_us[:, 0:128].indirect(ap(o)), ACT.Copy), [R("q_u", 0, 128), o], [R("uls", a, a + 256)], 0.45)
-        run("v", lambda e, a=a, o=o: e.tensor_copy(T.ul[:, a:a + 256].bitcast(dt.uint32), T.q_u[:, 0:128].bitcast(dt.uint32).indirect(ap(o))), [R("q_u", 0, 128), o], [R("ul", a, a + 256)], 0.45)
+        run("s", lambda e, a=a, o=o: e.activation(T.uls[:, a:a + 256], T.q_us[:, 0:128].indirect(ap(o)), ACT.Copy), [R("q_u", 0, 128), o], [R("uls", a, a + 256)], 0.4)
+        run("v", lambda e, a=a, o=o: e.tensor_copy(T.ul[:, a:a + 256].bitcast(dt.uint32), T.q_u[:, 0:128].bitcast(dt.uint32).indirect(ap(o))), [R("q_u", 0, 128), o], [R("ul", a, a + 256)], 0.4)
     quant("q_x", 0, C, "X0", 0)
+    fill(R("ones", 0, 528), 1.0)
+    fill(R("LP0", 0, C), NONE0)
+    scan(R("cval", 0, C), R("ones", 0, C), R("ones", 0, C), -MID - 1, OP.add, OP.mult)
+
+    def scatter(k, a, b): cp(R("LP%d" % k, 0, 768, 1, R("lU%d" % k, a, b)), R("cval", 16 * a, 16 * b))
+    scatter(0, 0, 24)
 
     def widen(n):
         w = 16
@@ -233,81 +255,70 @@ def rank_program(g, core, T, topo):
             m = min(w, C - w)
             cp(R(n, w, w + m), R(n, 0, m))
             w += m
-    iota(R("pI", 0, 1), [[1, 1]], 0, 1)
     iota(R("v16", 0, 16), [[1, 16]], 128, -1)
     iota(R("nI", 0, 24), [[16, 24]], 0, 0)
     iota(R("v4", 0, 16), [[-4, 16]], 128, 1)
     iota(R("iotaF", 0, 768), [[1, 768]], 0, 0, True)
     gfill(R("oT", C, 1536), 0)
     gfill(R("CP0", 0, C), NONE1)
-    fill(R("ones", 0, 528), 1.0)
-    fill(R("LP0", 0, C), NONE0)
-    scan(R("cval", 0, C), R("ones", 0, C), R("ones", 0, C), -MID - 1, OP.add, OP.mult)
-    ts(R("p15", 0, 1), R("pI", 0, 1), 15, OP.bitwise_and)
-    cp(I15, R("p15", 0, 1))
-    ts(CORR, I15, 15.0, OP.is_lt, LIFT, OP.mult)
     ts(R("v16m", 0, 16), R("v16", 0, 16), 15, OP.bitwise_and)
     ts(R("t16", 0, 16), R("v16m", 0, 16), 0.0, OP.is_equal, RESET, OP.mult)
     ts(R("t16", 16, 32), R("v16m", 0, 16), 1.0, OP.is_equal, LIFT, OP.mult)
     tt(R("d16h", 0, 16), R("t16", 0, 16), R("t16", 16, 32), OP.add)
     ts(R("base", 0, 24), R("nI", 0, 24), I15, OP.add)
     widen("d16h")
-    for k, t in ((TH16, 384.0), (LPC, NONE0), (UC, NONE1)): lane(k, 1.0, t)
+    act(R("LR0", C, 768), R("iotaF", 0, 768, 1, W("lU0")), ACT.Copy)
+    act(R("aF", 0, C), R("LR0", C, 768, 1, R("colU", 12, 36)), ACT.Copy)
+    cp(W("rU"), W("rtI")); ts(SR, W("rtI"), CORR, OP.add)
+    for k, t in ((LPC, NONE0), (UC, NONE1)): lane(k, 1.0, t)
+    lane(NCORR, -1.0, 0.0)
     act(W("n16"), W("base"), ACT.Identity, 1.0, CORR)
     act(W("n2"), W("n16"), ACT.Copy, 1.0, -MID)
     act(W("base", 24), W("base"), ACT.Copy, 1.0, 384.0)
     sfill(R("sA1", 0, 16), 0.0)
     sfill(R("DA", 0, 504), 1.0)
     act(R("d16b", 0, C), R("d16h", 0, C), ACT.Copy, 2.0 ** -6)
-    for k, a, b in ((KAP, 1, 0.0), (NKAP, -1, 0.0), (KLO, 1, -0.5), (XA, 2, -1.5), (GB0, -1, -0.75), (KS, 768, 0.0), (KT, 100, 50.0),
+    for k, a, b in ((KAP, 1, 0.0), (NKAP, -1, 0.0), (XA, 2, -1.5), (GB0, -1, -0.75), (KS, 768, 0.0), (K384, 384, 0.0), (KT, 100, 50.0),
                     (X4, 8, -7.0), (X384, 8 * 384, -7.0 * 384)): lane(k, a * 2.0 ** -6, b)
     sfill(slot("DA", 0, 5), 0.0)
     sfill(slot("DB", 0, 4, 0, 96), 0.0)
     sfill(slot("EB", 2, 4, 0, 96), 0.0)
     for n in ("EB", "EC"): act(slot(n, 3, 4, 0, 48), R("base", 0, 48), ACT.Copy)
 
-    SL, SR = L16("s16", C, 768), L16("s16", 0, C)
-
     def parents(k):
-        cp(R("LP%d" % k, 0, 768, 1, W("lU%d" % k)), R("cval", 0, C))
         scan(R("lpS", 0, C), R("d16h", 0, C), R("LP%d" % k, 0, C))
         ts(W("lpU"), L16("lpS"), LPC, OP.subtract)
-
-    def columns(a):
-        n = 36 - (768 - a) // 16
-        s = L16("s16", a, 768)
-        ts(R("colW", n, 36), s, TH16, OP.is_ge, 384.0, OP.mult)
-        tt(R("colX", n, 36), s, R("colW", n, 36), OP.subtract)
-        ts(R("colU", n, 36), R("colX", n, 36), CORR, OP.subtract)
 
     def ways(d, e, l, c):
         tt(slot(d, 1), l, c, OP.subtract)
         act(slot(e, 1, 4, 24), slot(d, 1), ACT.Copy)
         act(slot(d, 1, 4, 24), slot(d, 1), ACT.Copy, -1.0, -384.0)
 
-    cp(W("lU0"), W("ltI"))
-    ts(SL, W("ltI"), CORR, OP.add)
-    columns(C)
-    parents(0)
-    act(R("LR0", C, 768), R("iotaF", 0, 768, 1, W("lU0")), ACT.Copy)
-
     bank = lambda k, n: R("psS", 512 * k, 512 * k + n)
 
-    def scores(a, b):
-        for k in range(4): mm(bank(k, b - a), "ul", 128 * k, "q_x", a, b - a)
+    def scores(a, b, ks):
+        for k in ks: mm(bank(k, b - a), "ul", 128 * k, "q_x", a, b - a)
 
     def sign1(a, b):
         act(R("sA1", 16 + a, 16 + b), bank(0, b - a), ACT.Sign)
-        ts(R("TB1", a, b), bank(1, b - a), 0.0, OP.is_le, 0.25, OP.mult)
+        if a == 0: ts(R("TB1", a, b), bank(1, b - a), 0.0, OP.is_le, 0.25, OP.mult)
+        else:
+            act(R("tb", 0, b - a), bank(1, b - a), ACT.Sign, -1.0, TINY)
+            act(R("TB1", a, b), R("tb", 0, b - a), ACT.Copy, 0.125, 0.125)
 
     def sign2(a, b): act(R("sA2", a, b), bank(2, b - a), ACT.Sign)
 
     def turns2(a, b):
         act(R("oT", 1536 + a, 1536 + b), bank(3, b - a), ACT.Sign, -1.0, TINY)
-        gcopy(R("oT", 1920 + a, 1920 + b), R("oT", 1536 + a, 1536 + b))
+        if b - a == C: act(R("oT", 1920 + a, 1920 + b), bank(3, b - a), ACT.Sign, -1.0, TINY)
+        else: gcopy(R("oT", 1920 + a, 1920 + b), R("oT", 1536 + a, 1536 + b))
 
     def halves(a):
         dma("g", T.XYh[:, a:a + 768], T.XYh[:, 1536 + a:2304 + a], [R("XYh", 1536 + a, 2304 + a), R("XYh", a, a + 768)], [R("XYh", a, a + 768)], 3.0, 1.0, accum_op=OP.add)
+
+    def fours(o, s, n, a, b):
+        scan(R(s, a, b), R("d4h", 0, b - a), R(n, a, b))
+        ts(R(o, a // 4, b // 4), R(s, a + 3, b, 4), 4.0, OP.mult, ADD4, OP.add)
 
     for k in range(3):
         p = T.cores[rank ^ STEP[k]]
@@ -315,18 +326,19 @@ def rank_program(g, core, T, topo):
         X, XN = "X%d" % (k % 2), "X%d" % (1 - k % 2)
         LRk, LRn, lU = "LR%d" % k, "LR%d" % (k + 1), "lU%d" % k
         a0, b0 = (0, C) if k == 0 else (0, HALF)
-        scores(a0, b0)
+        scores(a0, b0, range(4))
         sign1(a0, b0)
+        if k == 0: parents(0)
         tt(R("oT", 0, C), R("TB1", 0, C, 1, R("colU", 12, 36)), R("sA1", 16, 16 + C), OP.add)
         if k == 0:
-            act(R("aF", 0, C), R(LRk, C, 768, 1, R("colU", 12, 36)), ACT.Copy)
+            act(R("LR0", 768, 1152), R("iotaF", 0, 768, 1, W("rU")), ACT.Copy)
             sign2(a0, b0)
         act(R("hpF", 0, C), R("sA1", 0, 16 + C, 1, W("lpU")), ACT.Copy, -1.0)
-        if k == 0: turns2(a0, b0)
-        act(R("GA", 0, C), R("oT", 0, 768, 1, W(lU)), ACT.Identity, -1.0, GB0)
         if k:
             sign2(a0, b0)
-            act(R("aF", 0, C), R(LRk, C, 768, 1, R("colU", 12, 36)), ACT.Copy)
+            turns2(a0, b0)
+        act(R("GA", 0, C), R("oT", 0, 768, 1, W(lU)), ACT.Identity, -1.0, GB0)
+        if k: act(R("aF", 0, C), R(LRk, C, 768, 1, R("colU", 12, 36)), ACT.Copy)
         scan(R("oS", C, 768), R("d16b", 0, C), R("hpF", 0, C))
         scan(R("oS", 0, C), R("d16b", 0, C), R("oT", 0, C))
         scan(R("s2S", 0, C), R("d16b", 0, C), R("sA2", 0, C))
@@ -337,14 +349,12 @@ def rank_program(g, core, T, topo):
         act(slot("EA", 3, 5), L16("s2S"), ACT.Relu, -768.0, KS)
         scan(R("aS", 0, C), R("d16h", 0, C), R("aF", 0, C))
         tt(slot("DA", 1, 5), L16("aS"), SL, OP.subtract)
-        if k == 0:
-            cp(W("rU"), W("rtI")); ts(SR, W("rtI"), CORR, OP.add)
         tt(W("RL"), SR, SL, OP.subtract)
-        ts(slot("EA", 2, 5), SL, CORR, OP.subtract)
+        act(slot("EA", 2, 5), SL, ACT.Identity, 1.0, NCORR)
         tt(slot("EA", 0, 5), L16("gS"), W("T0"), OP.is_gt)
         tt(slot("EA", 1, 5), W("ct"), W("RL"), OP.mult)
         ts(slot("EA", 4, 5), L16("s2S"), KAP, OP.is_equal, 768.0, OP.mult)
-        if k: turns2(a0, b0)
+        if k == 0: turns2(a0, b0)
         chain("OA", "DA", "EA", 120)
         cp(W("iN"), slot("OA", 3, 5))
         act(R("oT", 0, C), R("oT", 768, 2304, 1, W("iN")), ACT.Copy)
@@ -352,8 +362,7 @@ def rank_program(g, core, T, topo):
         act(R("GB", 0, C), R("oT", 0, 1536, 1, W("iP")), ACT.Copy)
         ways("DB", "EB", SL, W("n16"))
         tt(W("PK"), L16("lpS"), W("n2"), OP.subtract)
-        act(slot("EB", 0), slot("EA", 0, 5), ACT.Copy)
-        act(slot("EB", 0, 4, 24), slot("EA", 0, 5), ACT.Copy)
+        for a in (0, 24): tt(slot("EB", 0, 4, a), L16("gS"), W("T0"), OP.is_gt)
         act(slot("EB", 1), W("x0"), ACT.Relu, -1536.0, X384)
         ts(W("ca"), W("x0"), XA, OP.is_lt)
         tt(slot("EB", 2, 4, 24), W("ca"), W("PK"), OP.mult)
@@ -361,32 +370,27 @@ def rank_program(g, core, T, topo):
         chain("OB", "DB", "EB", 192)
         cp(R("sg1U", 0, 48), slot("OB", 3, 4, 0, 48))
         cp(R("CP%d" % k, 0, 1536, 1, W("iP")), R("cval", 0, C))
-        if k == 0: act(R("LR0", 768, 1152), R("iotaF", 0, 768, 1, W("rU")), ACT.Copy)
         act(R("LM", C, 768), R(LRk, C, 1152, 1, W("sg1U", 24)), ACT.Copy)
-        act(R("LM", 0, C), R(LRk, C, 1152, 1, W("sg1U")), ACT.Copy)
         scan(R("o2S", 0, C), R("d16b", 0, C), R("oT", 0, C))
+        scan(R("g2S", 0, C), R("d16b", 0, C), R("GB", 0, C))
         scan(R("cS", 0, C), R("d16h", 0, C), R("CP%d" % k, 0, C))
         ts(W("Tc"), L16("o2S"), KAP, OP.is_equal, 4096.0, OP.mult)
         ts(W("u1"), L16("cS"), UC, OP.subtract)
-        scan(R("g2S", 0, C), R("d16b", 0, C), R("GB", 0, C))
-        tt(W("ca1"), W("u1"), W("Tc"), OP.is_gt)
         tt(W("PK1"), L16("cS"), W("n2"), OP.subtract)
-        ts(W("N2"), L16("o2S"), KLO, OP.is_lt, 384.0, OP.mult)
-        tt(slot("EC", 2, 4, 24), W("ca1"), W("PK1"), OP.mult)
+        tt(W("ca1"), W("u1"), W("Tc"), OP.is_gt)
+        act(W("N2"), L16("o2S"), ACT.Relu, -384.0, K384)
         tt(slot("EC", 1), W("u1"), W("N2"), OP.min)
-        if OPT["sflags"]:
-            act(slot("EC", 0), L16("g2S"), ACT.Relu, -1.0, KAP)
-            act(slot("EC", 0, 4, 24), L16("g2S"), ACT.Relu, -1.0, KAP)
-            act(slot("DC", 2, 4, 24), L16("g2S"), ACT.Abs, 1.0, NKAP)
-        else:
-            ts(slot("EC", 0), L16("g2S"), KLO, OP.is_lt)
-            ts(slot("EC", 0, 4, 24), L16("g2S"), KLO, OP.is_lt)
-            ts(slot("DC", 2, 4, 24), L16("g2S"), KAP, OP.not_equal)
+        tt(slot("EC", 2, 4, 24), W("ca1"), W("PK1"), OP.mult)
+        for a in (0, 24): act(slot("EC", 0, 4, a), L16("g2S"), ACT.Relu, -1.0, KAP)
+        act(slot("DC", 2, 4, 24), L16("g2S"), ACT.Abs, 1.0, NKAP)
+        act(R("LM", 0, C), R(LRk, C, 1152, 1, W("sg1U")), ACT.Copy)
         ways("DC", "EC", slot("OA", 2, 5), W("base"))
         chain("OC", "DC", "EC", 192)
         cp(R("sgU", 0, 48), slot("OC", 3, 4, 0, 48))
-        cp(R("R3h", 0, C), R("LM", 0, 768, 1, W("sgU", 24)))
-        act(R("L3h", 0, C), R("LM", 0, 768, 1, W("sgU")), ACT.Copy)
+        cp(R("R3h", 0, HALF), R("LM", 0, 768, 1, R("sgU", 24, 36)))
+        act(R("L3h", 0, HALF), R("LM", 0, 768, 1, R("sgU", 0, 12)), ACT.Copy)
+        act(R("R3h", HALF, C), R("LM", 0, 768, 1, R("sgU", 36, 48)), ACT.Copy)
+        act(R("L3h", HALF, C), R("LM", 0, 768, 1, R("sgU", 12, 24)), ACT.Copy)
         if k == 0:
             ts(R("p3", 0, 1), R("pI", 0, 1), 3, OP.bitwise_and)
             cp(I3, R("p3", 0, 1))
@@ -398,66 +402,72 @@ def rank_program(g, core, T, topo):
             ts(ADD4, C12, -4.0, OP.mult, I3, OP.add)
             act(TH4, C12, ACT.Copy, 1.0, 384.0)
             widen("d4h")
-            for a in range(0, 1536, 256): act(R("XYh", 1536 + a, 1792 + a), R("LV", a, a + 256), ACT.Copy, 0.5)
-            for a in range(0, 1536, 256): ts(R("XYh", a, a + 256), R("X0", a, a + 256), 0.5, OP.mult)
-        scan(R("sR4", 0, C), R("d4h", 0, C), R("R3h", 0, C))
-        ts(R("oR", 0, 96), R("sR4", 3, C, 4), 4.0, OP.mult, ADD4, OP.add)
-        cuts = OPT["pieces"]
-        PIECES = list(zip(cuts, cuts[1:]))
-        for a, b in PIECES:
-            act(R("Rg", 4 * a, 4 * b), R("XYh", 0, 3072, 1, R("oR", a // 4, b // 4)), ACT.Copy)
+            for a in range(0, OPT["yS"], 128): act(R("XYh", 1536 + a, 1664 + a), R("LV", a, a + 128), ACT.Copy, 0.5)
+            for a in range(0, 1536, 128): ts(R("XYh", a, a + 128), R("X0", a, a + 128), 0.5, OP.mult)
+            for a in range(OPT["yS"], 1536, 128): ts(R("XYh", 1536 + a, 1664 + a), R("LV", a, a + 128), 0.5, OP.mult)
+        pieces = list(zip(OPT["pieces"], OPT["pieces"][1:]))
+
+        def right(part):
+            fours("oR", "sR4", "R3h", HALF * part, HALF * part + HALF)
+            for a, b in pieces:
+                if a // HALF == part: act(R("Rg", 4 * a, 4 * b), R("XYh", 0, 3072, 1, R("oR", a // 4, b // 4)), ACT.Copy)
+
+        def lists(a, b, sem, lat, part): remote(p, ap(R("rin%d" % k, a, b)), ap(R("rU%d" % k, a, b)), [R("rU%d" % k, a, b)], sem, R("rin%d" % k, a, b), lat, part)
+        right(0)
         scan(R("s16", 0, HALF), R("d16h", 0, HALF), R("R3h", 0, HALF))
-        scan(R("sL4", 0, C), R("d4h", 0, C), R("L3h", 0, C))
+        fours("oL", "sL4", "L3h", 0, HALF)
         ts(R("rU%d" % k, 0, 12), L16("s16", 0, HALF), CORR, OP.subtract)
-        ts(R("oL", 0, 96), R("sL4", 3, C, 4), 4.0, OP.mult, ADD4, OP.add)
-        gcopy(R(LRn, C, 768), R("L3h", 0, C))
-        remote(p, T["rin%d" % k][:, :], ap(R("rU%d" % k, 0, 12)), [R("rU%d" % k, 0, 12)], "ar%d" % k, R("rin%d" % k, 0, 12), OPT["list"] + (1.5 if k == 0 else 0), 0)
+        two = k < OPT["two"]
+        if two: lists(0, 12, "ar%d" % k, OPT["list"] + OPT["first"], 0)
+        right(1)
         scan(R("s16", C, 768), R("d16h", 0, C), R("L3h", 0, C))
         ts(W("lU%d" % (k + 1)), SL, CORR, OP.subtract)
-        remote(p, T["lin%d" % k][:, :], ap(W("lU%d" % (k + 1))), [W("lU%d" % (k + 1))], "al%d" % k, W("lin%d" % k), OPT["list"] + (1.0 if k == 0 else 0), 1)
+        if two: lists(12, 36, "al%d" % k, OPT["list"] + 0.4, 1)
+        else: lists(0, 36, "al%d" % k, OPT["list"], None)
+        for a in (0, HALF): gcopy(R(LRn, C + a, C + a + HALF), R("L3h", a, a + HALF))
         gcopy(R(LRn, 0, C), R("L3h", 0, C))
+        for n, (a, b) in enumerate(pieces):
+            if n == 1: fours("oL", "sL4", "L3h", HALF, C)
+            tt(R("Z", 4 * a, 4 * b), R("XYh", 0, 3072, 1, R("oL", a // 4, b // 4)), R("Rg", 4 * a, 4 * b), OP.add)
+            if b % 128 == 0: quant("q_z", b - 128, b, "Z", b - 128)
+        if k == 0: iota(R("imod", 0, 768), [[0, 2], [1, 384]], 0, 0, True)
         for c in range(3):
-            for a, b in PIECES:
-                if (b - 1) // 128 == c: tt(R("Z", 4 * a, 4 * b), R("XYh", 0, 3072, 1, R("oL", a // 4, b // 4)), R("Rg", 4 * a, 4 * b), OP.add)
-            quant("q_z", 128 * c, 128 * c + 128, "Z", 128 * c)
-        for c in range(3):
+            if c == 1:
+                act(R("mF", 0, HALF), R(LRn, 0, 768, 1, R("rin%d" % k, 0, 12)), ACT.Copy)
+                scan(R("mS", 0, HALF), R("d4h", 0, HALF), R("mF", 0, HALF))
+                m4 = R("mS", 3, HALF, 4)
+                ts(R("mm", 0, 48), m4, TH4, OP.is_ge, -1536.0, OP.mult)
+                act(R("mo", 0, 48), m4, ACT.Identity, 4.0, ADD4)
+                tt(R("ms", 0, 48), R("mm", 0, 48), R("mo", 0, 48), OP.add)
+                cp(R("mfU", 0, 48), R("ms", 0, 48))
+            if c == 2:
+                scan(R("s16", HALF, C), R("d16h", 0, HALF), R("R3h", HALF, C))
+                columns(L16("s16", HALF, 768), 12, 48, R("colU", 0, 36))
+                act(R("LPp", 0, C), R("imod", 0, 768, 1, W("lin%d" % k)), ACT.Copy)
             for b in range(4):
                 o = R("psS" if c == 1 else "psH", 512 * b, 512 * b + 128)
                 h = R("H", 512 * c + b, 512 * c + 512, 4)
                 mm(o, "q_w", 128 * b, "q_z", 128 * c, 128)
-                if c == 2 and b % 2 == 0 and b < 2 * OPT["hv"]: ts(h, o, 0.03125, OP.mult)
+                if 4 * c + b in OPT["hv"]: ts(h, o, 0.03125, OP.mult)
                 else: act(h, o, ACT.Copy, 0.03125)
-        pick(OPT["mfs"], R("mF", 0, HALF), R(LRn, 0, 768, 1, R("rin%d" % k, 0, 12)))
-        scan(R("mS", 0, HALF), R("d4h", 0, HALF), R("mF", 0, HALF))
-        m4 = R("mS", 3, HALF, 4)
-        ts(R("mm", 0, 48), m4, TH4, OP.is_ge, -1536.0, OP.mult)
-        act(R("mo", 0, 48), m4, ACT.Identity, 4.0, ADD4)
-        tt(R("ms", 0, 48), R("mm", 0, 48), R("mo", 0, 48), OP.add)
-        cp(R("mfU", 0, 48), R("ms", 0, 48))
         fs = OPT["fsplit"]
         cp(R("F", 0, 16 * fs), R("H", 0, 1536, 1, R("mfU", 0, fs)))
         act(R("F", 16 * fs, 768), R("H", 0, 1536, 1, R("mfU", fs, 48)), ACT.Copy)
         quant("fq%d" % k, 0, HALF, "F", 0)
-        remote(p, T["cin%d" % k][:, 0:HALF].bitcast(dt.uint8), T["fq%d" % k][:, 0:HALF].bitcast(dt.uint8), [R("fq%d" % k, 0, HALF)], "ac%d" % k, R("cin%d" % k, 0, HALF), OPT["far"])
-        remote(p, T["sin%d" % k][:, 0:HALF], T["fs%d" % k][:, 0:HALF], [R("fq%d" % k, 0, HALF)], "as%d" % k, R("sin%d" % k, 0, HALF), OPT["far"])
+        far = OPT["far"] - (k == 0) * OPT["on"]
+        remote(p, T["cin%d" % k][:, 0:HALF].bitcast(dt.uint8), T["fq%d" % k][:, 0:HALF].bitcast(dt.uint8), [R("fq%d" % k, 0, HALF)], "ac%d" % k, R("cin%d" % k, 0, HALF), far)
+        remote(p, T["sin%d" % k][:, 0:HALF], T["fs%d" % k][:, 0:HALF], [R("fq%d" % k, 0, HALF)], "as%d" % k, R("sin%d" % k, 0, HALF), far)
         gcopy(R(LRn, 768, 1152), R("R3h", 0, C))
         if k == 0:
-            iota(R("imod", 0, 768), [[0, 2], [1, 384]], 0, 0, True)
             run("g", lambda e: e.affine_select(T.E[:, 0:528], T.ones[:, 0:528], [[1, 528]], OP.is_equal, 0.0, -3, -4), [R("ones", 0, 528)], [R("E", 0, 528)], 1.2)
         if not last:
             gfill(R("LP%d" % (k + 1), 0, C), NONE0)
             gfill(R("CP%d" % (k + 1), 0, C), NONE1)
-        scan(R("s16", HALF, C), R("d16h", 0, HALF), R("R3h", HALF, C))
-        columns(HALF)
-        act(R("LPp", 0, C), R("imod", 0, 768, 1, W("lin%d" % k)), ACT.Copy)
         act(R("nF", 0, HALF), R("LPp", 0, C, 1, R("colU", 0, 12)), ACT.Copy)
+        fours("mnU", "mnS", "nF", 0, HALF)
         if last: dma("y", T.gr[:, :], T[LRn][0:128:16, C:], [R(LRn, C, 1152)], [])
-        if not last and OPT["lp"] == 0: parents(k + 1)
-        scan(R("mnS", 0, HALF), R("d4h", 0, HALF), R("nF", 0, HALF))
-        ts(R("mnU", 0, 48), R("mnS", 3, HALF, 4), 4.0, OP.mult, ADD4, OP.add)
         tt(R(XN, 768, 1536), R("H", 0, 1536, 1, R("mnU", 0, 48)), R(X, 768, 1536), OP.add)
         quant("q_x", HALF, C, XN, HALF)
-        if not last and OPT["lp"] == 1: parents(k + 1)
         if k == 0:
             for b in range(4): quant("q_e", 128 * b, 128 * b + 128, "E", 0, 3 - b)
         if last: quant("q_v", 0, 128, "vt", 0)
@@ -469,23 +479,27 @@ def rank_program(g, core, T, topo):
             dma("y" if a else "s", T.y[:, a:a + HALF], T.yS[:, a:a + HALF], [R("yS", a, a + HALF)], [])
             dma("y", T.oc[:, 4 * a:4 * a + 4 * HALF], T.q_x[:, a:a + HALF].bitcast(dt.uint8), [R("q_x", a, a + HALF)], [])
             for i in range(4):
-                dma("y", T.osc[4 * i:4 * i + 4, a:a + HALF], T.q_xs[32 * i:32 * i + 4, a:a + HALF], [R("q_x", a, a + HALF)], [])
+                dma("y" if a or i < 2 else "s", T.osc[4 * i:4 * i + 4, a:a + HALF], T.q_xs[32 * i:32 * i + 4, a:a + HALF], [R("q_x", a, a + HALF)], [])
         if not last:
-            scores(HALF, C)
+            scores(HALF, C, (0, 1))
             sign1(HALF, C)
-            sign2(HALF, C)
-            turns2(HALF, C)
             act(R("XYh", 2304, 3072), R("H", 0, 1536, 1, R("mnU", 0, 48)), ACT.Copy, 0.5)
             halves(768)
         else:
             finish(HALF)
         for b in range(4):
             mm(R("psH", 512 * b, 512 * b + HALF), "q_e", 128 * b, "cin%d" % k, 0, HALF, "sin%d" % k)
+        if not last:
+            scores(HALF, C, (2, 3))
+            sign2(HALF, C)
+            turns2(HALF, C)
         for b in range(4):
             tt(R(XN, b, 768, 4), R(X, b, 768, 4), R("psH", 512 * b, 512 * b + HALF), OP.add)
         quant("q_x", 0, HALF, XN, 0)
         if last: finish(0)
         else:
+            for a in range(0, 24, OPT["lpn"]): scatter(k + 1, a, a + OPT["lpn"])
+            parents(k + 1)
             for b in range(4): act(R("XYh", 1536 + b, 2304, 4), R("psH", 512 * b, 512 * b + HALF), ACT.Copy, 0.5)
             halves(0)
     emit()

from concourse.mybir import dt, AluOpType, ActivationFunctionType

C, HALF, STEP = 384, 192, [1, 2, 4]
OP, ACT = AluOpType, ActivationFunctionType
RESET, LIFT = -4096.0, 1024.0
TINY = 2.0 ** -101
MID, NONE0, NONE1 = 192.0, -208.0, -576.0
CY = 0.00085
OPT = {"wake": 0.14, "room": 0.15, "list": 2.1, "first": 1.2, "far": 2.0, "on": 0.5, "pe": 0.00125,
       "pieces": (0, 64, 128, 192, 256, 384), "hv": (8, 9, 10, 11), "yS": 1024, "lpn": 24, "two": 1, "fsplit": 24}

SCRATCH = {}
PLACE = {}


def _sb(n, w, t): SCRATCH[n] = ("sbuf", [128, w], t)


def _share(buf, t, items):
    at = 0
    for n, w in items:
        PLACE[n] = (buf, at); at += (w + 7) // 8 * 8
    _sb(buf, at, t)


for _n, _w in (("X0", 1536), ("X1", 1536), ("LV", 1536), ("XYh", 3072), ("H", 1536), ("Z", 1536), ("Rg", 1536), ("F", 768),
               ("ut", 512), ("vt", 512), ("E", 528), ("ones", 528), ("sA1", 16 + C), ("sA2", C), ("TB1", C), ("tb", HALF),
               ("oT", 2304), ("hpF", C), ("GA", C), ("GB", C), ("oS", 768), ("gS", C), ("s2S", C), ("o2S", C), ("g2S", C),
               ("d16b", C), ("cval", C)):
    _sb(_n, _w, "bfloat16")
for _n, _w in (("iotaF", 768), ("imod", 768), ("LPp", C), ("LM", 768), ("yS", C)):
    _sb(_n, _w, "float32")
for _n, _w in (("mF", HALF), ("mS", HALF), ("nF", HALF), ("mnS", HALF), ("d4h", C), ("d16h", C), ("L3h", C), ("R3h", C),
               ("sR4", C), ("sL4", C), ("s16", 768), ("aF", C), ("aS", C), ("lpS", C), ("cS", C)):
    _sb(_n, _w, "float16")
_share("wf", "float32", (("cst", 32), ("base", 48), ("n16", 24), ("n2", 24), ("t16", 32), ("u16", 32), ("colW", 48), ("colX", 48), ("RL", 24), ("PK", 24), ("x0", 24),
                         ("ct", 24), ("ca", 24), ("T0", 24), ("N2", 24), ("Tc", 24), ("u1", 24), ("ca1", 24), ("PK1", 24), ("mm", 48), ("mo", 48), ("ms", 48)))
_share("wh", "float16", (("DA", 120), ("DB", 192), ("DC", 192), ("EB", 192), ("EC", 192), ("EA", 120), ("OA", 120), ("OB", 192), ("OC", 192)))
_share("wi", "int32", (("pI", 1), ("p15", 1), ("p3", 1), ("v16", 16), ("v16m", 16), ("v4", 16), ("v4m", 16), ("nI", 24), ("uI", 32)))
_share("wu", "uint16", [("rU%d" % _k, 36) for _k in range(3)] +
       [("lU0", 24), ("rU", 24), ("colU", 40), ("lpU", 24), ("iP", 24), ("iN", 24), ("sgU", 48), ("sg1U", 48), ("oR", 96), ("oL", 96), ("mfU", 48), ("mnU", 48), ("uU", 32)])
_sb("ltI", 24, "int32"); _sb("rtI", 24, "int32")
for _k in range(3):
    PLACE["lU%d" % (_k + 1)] = ("wu", PLACE["rU%d" % _k][1] + 12)
    PLACE["lin%d" % _k] = ("rin%d" % _k, 12)
    _sb("rin%d" % _k, 36, "uint16")
    _sb("LP%d" % _k, 768, "bfloat16"); _sb("CP%d" % _k, 1536, "bfloat16")
    _sb("fq%d" % _k, HALF, "float8_e4m3fn_x4"); _sb("fs%d" % _k, HALF, "uint8")
    _sb("cin%d" % _k, HALF, "float8_e4m3fn_x4"); _sb("sin%d" % _k, HALF, "uint8")
for _k in range(4): _sb("LR%d" % _k, 3 * C, "float32")
for _n, _w in (("q_u", 128), ("ul", 512), ("q_v", 128), ("q_e", 512), ("q_w", 512), ("q_x", C), ("q_z", C)):
    _sb(_n, _w, "float8_e4m3fn_x4"); _sb(_n + "s", _w, "uint8")
SCRATCH["psS"] = ("psum", [128, 2048], "float32")
SCRATCH["psH"] = ("psum", [128, 2048], "float32")
SEMAPHORES = ["cv", "cs", "cp", "cg", "left"] + ["d%d" % _i for _i in range(40)] + ["a%s%d" % (_n, _k) for _n in ("r", "l", "c", "s") for _k in range(3)]


def R(n, a, b, st=1, off=None):
    n, at = PLACE.get(n, (n, 0))
    return (n, at + a, at + b, st, off)


def W(n, a=0): return R(n, a, a + 24)


def L16(n, a=0, b=C): return R(n, a + 15, b, 16)


def slot(n, s, of=4, a=0, k=24): return R(n, of * a + s, of * (a + k), of)


def rank_program(g, core, T, topo):
    rank = T.rank_of(core)
    if rank is None:
        return
    ops = []
    hist = {}
    ndma = [0]
    WAKE = OPT["wake"]

    def meet(r, o):
        if r[0].startswith("ps"): return r[1] // 512 == o[1] // 512
        if r[2] <= o[1] or o[2] <= r[1]: return False
        return not (r[3] == o[3] and r[3] > 1 and (r[1] - o[1]) % r[3])

    def add(q, fn, reads, writes, t, sem, n, lat=0.0):
        i, wait, order = len(ops), set(), set()
        compute = sem[0] == "c"
        for isw, rs in ((False, reads), (True, writes)):
            for r in rs:
                for w0, o, c in hist.get(r[0], ()):
                    if not (isw or w0 or r[0].startswith("ps")) or not meet(r, o): continue
                    if isw and not w0 and compute and ops[c]["q"] == q and ops[c]["sem"] == sem: order.add(c)
                    else: wait.add(c)
        ops.append({"q": q, "fn": fn, "wait": wait, "order": order - wait, "t": t, "sem": sem, "n": n, "lat": lat})
        c = i
        for r in writes:
            h = hist.setdefault(r[0], [])
            if not r[0].startswith("ps"):
                h[:] = [e for e in h if not (r[3] == 1 and r[1] <= e[1][1] and e[1][2] <= r[2])]
            else:
                h[:] = [e for e in h if e[1][1] // 512 != r[1] // 512]
            h.append((True, r, c))
        for r in reads: hist.setdefault(r[0], []).append((False, r, c))
        return i

    def emit():
        busy = {}
        for o in ops:
            t0 = max([0.0] + [ops[c]["end"] + ops[c]["lat"] + WAKE for c in o["wait"]] + [ops[c]["end"] for c in o["order"]])
            if o["q"] != "far":
                held = busy.setdefault(o["q"], [])
                n = 0
                for n, (x, y) in enumerate(held + [(1e9, 1e9)]):
                    if t0 + o["t"] * (1 - OPT["room"]) <= x + 1e-9 and t0 < x: break
                    t0 = max(t0, y)
                held.insert(n, (t0, t0 + o["t"]))
            o["start"], o["end"] = t0, t0 + o["t"]
        OPT["est"] = max(o["end"] + o["lat"] for o in ops)
        eng = {"v": g.vector, "s": g.scalar, "p": g.tensor, "g": g, "y": g.sync}
        count = {"left": 0}
        known = {q: {} for q in eng}
        for o in sorted(ops, key=lambda o: o["start"]):
            q, sem = o["q"], o["sem"]
            if q == "far":
                count[sem] = o["n"]
                o["vc"], o["at"] = {sem: o["n"]}, o["n"]
                continue
            need = [ops[c] for c in sorted(o["wait"]) if known[q].get(ops[c]["sem"], 0) < ops[c]["at"]]
            keep = {}
            for c in need:
                if any(d["vc"].get(c["sem"], 0) >= c["at"] and (d["sem"], d["at"]) != (c["sem"], c["at"]) for d in need): continue
                keep[c["sem"], c["at"]] = c
            for (s, n), c in keep.items():
                eng[q].wait_ge(T.sem[s], n)
                for s, n in c["vc"].items(): known[q][s] = max(known[q].get(s, 0), n)
            count[sem] = count.get(sem, 0) + o["n"]
            inst = o["fn"](eng[q])
            if sem != "left": inst.then_inc(T.sem[sem], o["n"])
            o["at"] = count[sem]
            o["vc"] = dict(known[q]); o["vc"][sem] = count[sem]
        for s in sorted(count): g.wait_ge(T.sem[s], count[s])

    def width(r): return 16 * (r[4][2] - r[4][1]) if r[4] else -(-(r[2] - r[1]) // r[3])
    def half(*rs): return all(SCRATCH[r[0]][2] in ("bfloat16", "float16", "uint16") for r in rs)
    def plain(n): return max(64, n) * CY
    def picked(o, a): return 0.05 + width(o) * 3.8 * CY if o[4] else 0.06 + width(a) * 1.56 * CY

    def run(q, fn, reads, writes, t=1.0):
        rd = []
        for r in list(reads) + [r[4] for r in writes if r[4]]:
            rd.append(r)
            if r[4]: rd.append(r[4])
        w = list(writes) + [r for r in rd if r[0].startswith("ps")]
        rd = [r for r in rd if not r[0].startswith("ps")]
        add(q, fn, rd, w, t, "c" + q, 1)

    def dma(q, out, in_, reads, writes, lat=2.0, hold=0.06, **kw):
        sem = "d%d" % ndma[0]; ndma[0] += 1
        add(q, lambda e: e.dma_start(out, in_, **kw), reads, writes, hold, sem, 16, lat)

    def ap(r):
        n, a, b, st, off = r
        v = T[n][:, a:b] if st == 1 else T[n][:, a:b:st]
        if off is not None: v = v.indirect(T[off[0]][:, off[1]:off[2]])
        return v

    def tt(o, a, b, op):
        t = picked(o, a) if a[4] else plain(width(o) * (1 if "ps" in (a[0][:2], b[0][:2]) else 2))
        run("v", lambda e: e.tensor_tensor(ap(o), ap(a), ap(b), op), [a, b], [o], t)
    def ts(o, a, s1, op0, s2=None, op1=None):
        rs = [a] + [s for s in (s1, s2) if isinstance(s, tuple)]
        f = lambda s: ap(s) if isinstance(s, tuple) else s
        t = plain(width(o) * (0.5 if half(o, a) else 1))
        if op1 is None: run("v", lambda e: e.tensor_scalar(ap(o), ap(a), f(s1), None, op0), rs, [o], t)
        else: run("v", lambda e: e.tensor_scalar(ap(o), ap(a), f(s1), f(s2), op0, op1), rs, [o], t)
    def cp(o, a): run("v", lambda e: e.tensor_copy(ap(o), ap(a)), [a], [o], picked(o, a) if o[4] or a[4] else plain(width(o) * (0.5 if half(o, a) else 1)))
    def fill(o, c): run("v", lambda e: e.memset(ap(o), c), [], [o], plain(width(o) * (0.5 if half(o) else 1)))
    def scan(o, d, a, first=0.0, op0=OP.add, op1=OP.max):
        run("v", lambda e: e.tensor_tensor_scan(ap(o), ap(d), ap(a), first, op0, op1), [d, a], [o], plain(width(o) * (0.5 if half(o, d, a) else 1)))
    def chain(o, d, a, n): scan(R(o, 0, n), R(d, 0, n), R(a, 0, n), 0.0, OP.mult, OP.add)
    def act(o, a, f, scale=1.0, bias=0.0):
        kw = {n: x for n, x, d in (("scale", scale, 1.0), ("bias", bias, 0.0)) if x != d}
        kv = {n: ap(x) if isinstance(x, tuple) else x for n, x in kw.items()}
        run("s", lambda e: e.activation(ap(o), ap(a), f, **kv), [a] + [x for x in kw.values() if isinstance(x, tuple)], [o], picked(o, a) if a[4] else plain(width(o)))
    def sfill(o, c): act(o, R("ones", 0, width(o)), ACT.Copy, c)
    def quant(q, a, b, tile, ta, shift=0):
        i = R(tile, 4 * ta + shift, 4 * (ta + b - a) + shift)
        s = q.replace("fq", "fs") if q.startswith("fq") else q + "s"
        run("v", lambda e: e.quantize_mx(T[q][:, a:b], T[s][:, a:b], ap(i)), [i], [R(q, a, b)], 0.015 + 0.001 * (b - a))
    def mm(o, qa, a, qb, b, n, sb=None):
        s = sb or qb + "s"
        run("p", lambda e: e.matmul_mx(ap(o), T[qa][:, a:a + 128], T[qa + "s"][:, a:a + 128], T[qb][:, b:b + n], T[s][:, b:b + n], True, True),
            [R(n_, x, y) for n_, x, y in ((qa, a, a + 128), (qa + "s", a, a + 128), (qb, b, b + n), (s, b, b + n))], [o], (n + 16) * OPT["pe"])
    def iota(o, pat, base, cm, fl=False):
        run("g", lambda e: e.iota(ap(o), pat, base, cm, allow_small_or_imprecise_dtypes=True) if fl else e.iota(ap(o), pat, base, cm), [], [o], 0.15 + width(o) * 2 * CY)
    def gfill(o, c): iota(o, [[0, width(o)]], int(c), 0, True)
    def gcopy(o, a):
        run("g", lambda e: e.affine_select(ap(o), ap(a), [[0, width(o)]], OP.is_ge, 0.0, 0, 0), [a], [o], 0.2 + width(o) * 2 * CY)
    I15, I3, CORR, C12, ADD4, TH4, TH16, KAP, NKAP, NCORR, XA, GB0, KS, LPC, UC, KT, X4, X384, K384 = [R("cst", i, i + 1) for i in range(19)]

    def lane(k, a, b): act(k, CORR, ACT.Copy, a, b)

    def remote(dst, out, in_, reads, arr, land, lat, part=None):
        rid, pid, _ = topo.addr(dst)
        es = topo.engines(core, dst)
        if part is not None: es = es[part * len(es) // 2:(part + 1) * len(es) // 2]
        i = add("g", lambda e: e.remote_dma(out, in_, T.sem[arr], T.sem.left, pid, rid, sum(1 << n for n in es)), reads, [], 0.6, "left", len(es))
        j = add("far", None, [], [land], lat, arr, len(es))
        ops[j]["order"] |= {i}

    def load(q, n, src, a, b, bc=None, behind=(), lat=1.7):
        dma(q, T[n][:, a:b] if bc is None else T[n][:, a:b].bitcast(bc), src, list(behind), [R(n, a, b)], lat)
    load("y", "ut", T.u[:, :], 0, 512, lat=1.9)
    load("s", "ltI", T.lt[:, :], 0, 24)
    load("y", "X0", T.x[:, :], 0, 1536, lat=3.0)
    load("s", "rtI", T.rt[:, :], 0, 24)
    load("y", "LV", T.lv[:, :], 0, 1536, None, [R("ut", 0, 512)], 3.0)
    load("y", "q_w", T.wc[:, :], 0, 512, dt.uint8, [R("X0", 0, 1536)], 3.0)
    load("y", "q_ws", T.ws[:, :], 0, 512, None, [R("X0", 0, 1536)], 3.0)
    load("y", "vt", T.v[:, :], 0, 512, None, [R("X0", 0, 1536)], 3.0)

    SL, SR = L16("s16", C, 768), L16("s16", 0, C)

    def columns(s, a, b, o):
        ts(R("colW", a, b), s, TH16, OP.is_ge, 384.0, OP.mult)
        tt(R("colX", a, b), s, R("colW", a, b), OP.subtract)
        ts(o, R("colX", a, b), CORR, OP.subtract)
    iota(R("pI", 0, 1), [[1, 1]], 0, 1)
    iota(R("uI", 0, 32), [[1, 4], [16, 8]], 0, 0)
    ts(R("p15", 0, 1), R("pI", 0, 1), 15, OP.bitwise_and)
    cp(I15, R("p15", 0, 1))
    ts(CORR, I15, 15.0, OP.is_lt, LIFT, OP.mult)
    lane(TH16, 1.0, 384.0)
    cp(W("lU0"), W("ltI"))
    ts(SL, W("ltI"), CORR, OP.add)
    columns(SL, 24, 48, R("colU", 12, 36))
    cp(R("uU", 0, 32), R("uI", 0, 32))
    quant("q_u", 0, 128, "ut", 0)
    for a in (0, 256):
        o = R("uU", a // 16, a // 16 + 16)
        run("s", lambda e, a=a, o=o: e.activation(T.uls[:, a:a + 256], T.q_us[:, 0:128].indirect(ap(o)), ACT.Copy), [R("q_u", 0, 128), o], [R("uls", a, a + 256)], 0.4)
        run("v", lambda e, a=a, o=o: e.tensor_copy(T.ul[:, a:a + 256].bitcast(dt.uint32), T.q_u[:, 0:128].bitcast(dt.uint32).indirect(ap(o))), [R("q_u", 0, 128), o], [R("ul", a, a + 256)], 0.4)
    quant("q_x", 0, C, "X0", 0)
    fill(R("ones", 0, 528), 1.0)
    fill(R("LP0", 0, C), NONE0)
    scan(R("cval", 0, C), R("ones", 0, C), R("ones", 0, C), -MID - 1, OP.add, OP.mult)

    def scatter(k, a, b): cp(R("LP%d" % k, 0, 768, 1, R("lU%d" % k, a, b)), R("cval", 16 * a, 16 * b))
    scatter(0, 0, 24)

    def widen(n):
        w = 16
        while w < C:
            m = min(w, C - w)
            cp(R(n, w, w + m), R(n, 0, m))
            w += m
    iota(R("v16", 0, 16), [[1, 16]], 128, -1)
    iota(R("nI", 0, 24), [[16, 24]], 0, 0)
    iota(R("v4", 0, 16), [[-4, 16]], 128, 1)
    iota(R("iotaF", 0, 768), [[1, 768]], 0, 0, True)
    gfill(R("oT", C, 1536), 0)
    gfill(R("CP0", 0, C), NONE1)
    ts(R("v16m", 0, 16), R("v16", 0, 16), 15, OP.bitwise_and)
    ts(R("t16", 0, 16), R("v16m", 0, 16), 0.0, OP.is_equal, RESET, OP.mult)
    ts(R("t16", 16, 32), R("v16m", 0, 16), 1.0, OP.is_equal, LIFT, OP.mult)
    tt(R("d16h", 0, 16), R("t16", 0, 16), R("t16", 16, 32), OP.add)
    ts(R("base", 0, 24), R("nI", 0, 24), I15, OP.add)
    widen("d16h")
    act(R("LR0", C, 768), R("iotaF", 0, 768, 1, W("lU0")), ACT.Copy)
    act(R("aF", 0, C), R("LR0", C, 768, 1, R("colU", 12, 36)), ACT.Copy)
    cp(W("rU"), W("rtI")); ts(SR, W("rtI"), CORR, OP.add)
    for k, t in ((LPC, NONE0), (UC, NONE1)): lane(k, 1.0, t)
    lane(NCORR, -1.0, 0.0)
    act(W("n16"), W("base"), ACT.Identity, 1.0, CORR)
    act(W("n2"), W("n16"), ACT.Copy, 1.0, -MID)
    act(W("base", 24), W("base"), ACT.Copy, 1.0, 384.0)
    sfill(R("sA1", 0, 16), 0.0)
    sfill(R("DA", 0, 504), 1.0)
    act(R("d16b", 0, C), R("d16h", 0, C), ACT.Copy, 2.0 ** -6)
    for k, a, b in ((KAP, 1, 0.0), (NKAP, -1, 0.0), (XA, 2, -1.5), (GB0, -1, -0.75), (KS, 768, 0.0), (K384, 384, 0.0), (KT, 100, 50.0),
                    (X4, 8, -7.0), (X384, 8 * 384, -7.0 * 384)): lane(k, a * 2.0 ** -6, b)
    sfill(slot("DA", 0, 5), 0.0)
    sfill(slot("DB", 0, 4, 0, 96), 0.0)
    sfill(slot("EB", 2, 4, 0, 96), 0.0)
    for n in ("EB", "EC"): act(slot(n, 3, 4, 0, 48), R("base", 0, 48), ACT.Copy)

    def parents(k):
        scan(R("lpS", 0, C), R("d16h", 0, C), R("LP%d" % k, 0, C))
        ts(W("lpU"), L16("lpS"), LPC, OP.subtract)

    def ways(d, e, l, c):
        tt(slot(d, 1), l, c, OP.subtract)
        act(slot(e, 1, 4, 24), slot(d, 1), ACT.Copy)
        act(slot(d, 1, 4, 24), slot(d, 1), ACT.Copy, -1.0, -384.0)

    bank = lambda k, n: R("psS", 512 * k, 512 * k + n)

    def scores(a, b, ks):
        for k in ks: mm(bank(k, b - a), "ul", 128 * k, "q_x", a, b - a)

    def sign1(a, b):
        act(R("sA1", 16 + a, 16 + b), bank(0, b - a), ACT.Sign)
        if a == 0: ts(R("TB1", a, b), bank(1, b - a), 0.0, OP.is_le, 0.25, OP.mult)
        else:
            act(R("tb", 0, b - a), bank(1, b - a), ACT.Sign, -1.0, TINY)
            act(R("TB1", a, b), R("tb", 0, b - a), ACT.Copy, 0.125, 0.125)

    def sign2(a, b): act(R("sA2", a, b), bank(2, b - a), ACT.Sign)

    def turns2(a, b):
        act(R("oT", 1536 + a, 1536 + b), bank(3, b - a), ACT.Sign, -1.0, TINY)
        if b - a == C: act(R("oT", 1920 + a, 1920 + b), bank(3, b - a), ACT.Sign, -1.0, TINY)
        else: gcopy(R("oT", 1920 + a, 1920 + b), R("oT", 1536 + a, 1536 + b))

    def halves(a):
        dma("g", T.XYh[:, a:a + 768], T.XYh[:, 1536 + a:2304 + a], [R("XYh", 1536 + a, 2304 + a), R("XYh", a, a + 768)], [R("XYh", a, a + 768)], 3.0, 1.0, accum_op=OP.add)

    def fours(o, s, n, a, b):
        scan(R(s, a, b), R("d4h", 0, b - a), R(n, a, b))
        ts(R(o, a // 4, b // 4), R(s, a + 3, b, 4), 4.0, OP.mult, ADD4, OP.add)

    for k in range(3):
        p = T.cores[rank ^ STEP[k]]
        last = k == 2
        X, XN = "X%d" % (k % 2), "X%d" % (1 - k % 2)
        LRk, LRn, lU = "LR%d" % k, "LR%d" % (k + 1), "lU%d" % k
        a0, b0 = (0, C) if k == 0 else (0, HALF)
        scores(a0, b0, range(4))
        sign1(a0, b0)
        if k == 0: parents(0)
        tt(R("oT", 0, C), R("TB1", 0, C, 1, R("colU", 12, 36)), R("sA1", 16, 16 + C), OP.add)
        if k == 0:
            act(R("LR0", 768, 1152), R("iotaF", 0, 768, 1, W("rU")), ACT.Copy)
            sign2(a0, b0)
        act(R("hpF", 0, C), R("sA1", 0, 16 + C, 1, W("lpU")), ACT.Copy, -1.0)
        if k:
            sign2(a0, b0)
            turns2(a0, b0)
        act(R("GA", 0, C), R("oT", 0, 768, 1, W(lU)), ACT.Identity, -1.0, GB0)
        if k: act(R("aF", 0, C), R(LRk, C, 768, 1, R("colU", 12, 36)), ACT.Copy)
        scan(R("oS", C, 768), R("d16b", 0, C), R("hpF", 0, C))
        scan(R("oS", 0, C), R("d16b", 0, C), R("oT", 0, C))
        scan(R("s2S", 0, C), R("d16b", 0, C), R("sA2", 0, C))
        tt(W("x0"), L16("oS"), L16("oS", C, 768), OP.add)
        scan(R("gS", 0, C), R("d16b", 0, C), R("GA", 0, C))
        act(W("T0"), L16("oS"), ACT.Relu, -100.0, KT)
        act(W("ct"), W("x0"), ACT.Relu, -4.0, X4)
        act(slot("EA", 3, 5), L16("s2S"), ACT.Relu, -768.0, KS)
        scan(R("aS", 0, C), R("d16h", 0, C), R("aF", 0, C))
        tt(slot("DA", 1, 5), L16("aS"), SL, OP.subtract)
        tt(W("RL"), SR, SL, OP.subtract)
        act(slot("EA", 2, 5), SL, ACT.Identity, 1.0, NCORR)
        tt(slot("EA", 0, 5), L16("gS"), W("T0"), OP.is_gt)
        tt(slot("EA", 1, 5), W("ct"), W("RL"), OP.mult)
        ts(slot("EA", 4, 5), L16("s2S"), KAP, OP.is_equal, 768.0, OP.mult)
        if k == 0: turns2(a0, b0)
        chain("OA", "DA", "EA", 120)
        cp(W("iN"), slot("OA", 3, 5))
        act(R("oT", 0, C), R("oT", 768, 2304, 1, W("iN")), ACT.Copy)
        cp(W("iP"), slot("OA", 4, 5))
        act(R("GB", 0, C), R("oT", 0, 1536, 1, W("iP")), ACT.Copy)
        ways("DB", "EB", SL, W("n16"))
        tt(W("PK"), L16("lpS"), W("n2"), OP.subtract)
        for a in (0, 24): tt(slot("EB", 0, 4, a), L16("gS"), W("T0"), OP.is_gt)
        act(slot("EB", 1), W("x0"), ACT.Relu, -1536.0, X384)
        ts(W("ca"), W("x0"), XA, OP.is_lt)
        tt(slot("EB", 2, 4, 24), W("ca"), W("PK"), OP.mult)
        tt(slot("DB", 2, 4, 24), L16("gS"), W("T0"), OP.is_ge)
        chain("OB", "DB", "EB", 192)
        cp(R("sg1U", 0, 48), slot("OB", 3, 4, 0, 48))
        cp(R("CP%d" % k, 0, 1536, 1, W("iP")), R("cval", 0, C))
        act(R("LM", C, 768), R(LRk, C, 1152, 1, W("sg1U", 24)), ACT.Copy)
        scan(R("o2S", 0, C), R("d16b", 0, C), R("oT", 0, C))
        scan(R("g2S", 0, C), R("d16b", 0, C), R("GB", 0, C))
        scan(R("cS", 0, C), R("d16h", 0, C), R("CP%d" % k, 0, C))
        ts(W("Tc"), L16("o2S"), KAP, OP.is_equal, 4096.0, OP.mult)
        ts(W("u1"), L16("cS"), UC, OP.subtract)
        tt(W("PK1"), L16("cS"), W("n2"), OP.subtract)
        tt(W("ca1"), W("u1"), W("Tc"), OP.is_gt)
        act(W("N2"), L16("o2S"), ACT.Relu, -384.0, K384)
        tt(slot("EC", 1), W("u1"), W("N2"), OP.min)
        tt(slot("EC", 2, 4, 24), W("ca1"), W("PK1"), OP.mult)
        for a in (0, 24): act(slot("EC", 0, 4, a), L16("g2S"), ACT.Relu, -1.0, KAP)
        act(slot("DC", 2, 4, 24), L16("g2S"), ACT.Abs, 1.0, NKAP)
        act(R("LM", 0, C), R(LRk, C, 1152, 1, W("sg1U")), ACT.Copy)
        ways("DC", "EC", slot("OA", 2, 5), W("base"))
        chain("OC", "DC", "EC", 192)
        cp(R("sgU", 0, 48), slot("OC", 3, 4, 0, 48))
        cp(R("R3h", 0, HALF), R("LM", 0, 768, 1, R("sgU", 24, 36)))
        act(R("L3h", 0, HALF), R("LM", 0, 768, 1, R("sgU", 0, 12)), ACT.Copy)
        act(R("R3h", HALF, C), R("LM", 0, 768, 1, R("sgU", 36, 48)), ACT.Copy)
        act(R("L3h", HALF, C), R("LM", 0, 768, 1, R("sgU", 12, 24)), ACT.Copy)
        if k == 0:
            ts(R("p3", 0, 1), R("pI", 0, 1), 3, OP.bitwise_and)
            cp(I3, R("p3", 0, 1))
            ts(R("v4m", 0, 16), R("v4", 0, 16), 15, OP.bitwise_and)
            ts(R("u16", 0, 16), R("v4m", 0, 16), 4.0, OP.is_lt, RESET, OP.mult)
            ts(R("u16", 16, 32), R("v4m", 0, 16), 12.0, OP.is_ge, LIFT, OP.mult)
            tt(R("d4h", 0, 16), R("u16", 0, 16), R("u16", 16, 32), OP.add)
            ts(C12, I15, 12.0, OP.is_lt, LIFT, OP.mult)
            ts(ADD4, C12, -4.0, OP.mult, I3, OP.add)
            act(TH4, C12, ACT.Copy, 1.0, 384.0)
            widen("d4h")
            for a in range(0, OPT["yS"], 128): act(R("XYh", 1536 + a, 1664 + a), R("LV", a, a + 128), ACT.Copy, 0.5)
            for a in range(0, 1536, 128): ts(R("XYh", a, a + 128), R("X0", a, a + 128), 0.5, OP.mult)
            for a in range(OPT["yS"], 1536, 128): ts(R("XYh", 1536 + a, 1664 + a), R("LV", a, a + 128), 0.5, OP.mult)
        pieces = list(zip(OPT["pieces"], OPT["pieces"][1:]))

        def right(part):
            fours("oR", "sR4", "R3h", HALF * part, HALF * part + HALF)
            for a, b in pieces:
                if a // HALF == part: act(R("Rg", 4 * a, 4 * b), R("XYh", 0, 3072, 1, R("oR", a // 4, b // 4)), ACT.Copy)

        def lists(a, b, sem, lat, part): remote(p, ap(R("rin%d" % k, a, b)), ap(R("rU%d" % k, a, b)), [R("rU%d" % k, a, b)], sem, R("rin%d" % k, a, b), lat, part)
        right(0)
        scan(R("s16", 0, HALF), R("d16h", 0, HALF), R("R3h", 0, HALF))
        fours("oL", "sL4", "L3h", 0, HALF)
        ts(R("rU%d" % k, 0, 12), L16("s16", 0, HALF), CORR, OP.subtract)
        two = k < OPT["two"]
        if two: lists(0, 12, "ar%d" % k, OPT["list"] + OPT["first"], 0)
        right(1)
        scan(R("s16", C, 768), R("d16h", 0, C), R("L3h", 0, C))
        ts(W("lU%d" % (k + 1)), SL, CORR, OP.subtract)
        if two: lists(12, 36, "al%d" % k, OPT["list"] + 0.4, 1)
        else: lists(0, 36, "al%d" % k, OPT["list"], None)
        for a in (0, HALF): gcopy(R(LRn, C + a, C + a + HALF), R("L3h", a, a + HALF))
        gcopy(R(LRn, 0, C), R("L3h", 0, C))
        for n, (a, b) in enumerate(pieces):
            if n == 1: fours("oL", "sL4", "L3h", HALF, C)
            tt(R("Z", 4 * a, 4 * b), R("XYh", 0, 3072, 1, R("oL", a // 4, b // 4)), R("Rg", 4 * a, 4 * b), OP.add)
            if b % 128 == 0: quant("q_z", b - 128, b, "Z", b - 128)
        if k == 0: iota(R("imod", 0, 768), [[0, 2], [1, 384]], 0, 0, True)
        for c in range(3):
            if c == 1:
                act(R("mF", 0, HALF), R(LRn, 0, 768, 1, R("rin%d" % k, 0, 12)), ACT.Copy)
                scan(R("mS", 0, HALF), R("d4h", 0, HALF), R("mF", 0, HALF))
                m4 = R("mS", 3, HALF, 4)
                ts(R("mm", 0, 48), m4, TH4, OP.is_ge, -1536.0, OP.mult)
                act(R("mo", 0, 48), m4, ACT.Identity, 4.0, ADD4)
                tt(R("ms", 0, 48), R("mm", 0, 48), R("mo", 0, 48), OP.add)
                cp(R("mfU", 0, 48), R("ms", 0, 48))
            if c == 2:
                scan(R("s16", HALF, C), R("d16h", 0, HALF), R("R3h", HALF, C))
                columns(L16("s16", HALF, 768), 12, 48, R("colU", 0, 36))
                act(R("LPp", 0, C), R("imod", 0, 768, 1, W("lin%d" % k)), ACT.Copy)
            for b in range(4):
                o = R("psS" if c == 1 else "psH", 512 * b, 512 * b + 128)
                h = R("H", 512 * c + b, 512 * c + 512, 4)
                mm(o, "q_w", 128 * b, "q_z", 128 * c, 128)
                if 4 * c + b in OPT["hv"]: ts(h, o, 0.03125, OP.mult)
                else: act(h, o, ACT.Copy, 0.03125)
        fs = OPT["fsplit"]
        cp(R("F", 0, 16 * fs), R("H", 0, 1536, 1, R("mfU", 0, fs)))
        act(R("F", 16 * fs, 768), R("H", 0, 1536, 1, R("mfU", fs, 48)), ACT.Copy)
        quant("fq%d" % k, 0, HALF, "F", 0)
        far = OPT["far"] - (k == 0) * OPT["on"]
        remote(p, T["cin%d" % k][:, 0:HALF].bitcast(dt.uint8), T["fq%d" % k][:, 0:HALF].bitcast(dt.uint8), [R("fq%d" % k, 0, HALF)], "ac%d" % k, R("cin%d" % k, 0, HALF), far)
        remote(p, T["sin%d" % k][:, 0:HALF], T["fs%d" % k][:, 0:HALF], [R("fq%d" % k, 0, HALF)], "as%d" % k, R("sin%d" % k, 0, HALF), far)
        gcopy(R(LRn, 768, 1152), R("R3h", 0, C))
        if k == 0:
            run("g", lambda e: e.affine_select(T.E[:, 0:528], T.ones[:, 0:528], [[1, 528]], OP.is_equal, 0.0, -3, -4), [R("ones", 0, 528)], [R("E", 0, 528)], 1.2)
        if not last:
            gfill(R("LP%d" % (k + 1), 0, C), NONE0)
            gfill(R("CP%d" % (k + 1), 0, C), NONE1)
        act(R("nF", 0, HALF), R("LPp", 0, C, 1, R("colU", 0, 12)), ACT.Copy)
        fours("mnU", "mnS", "nF", 0, HALF)
        if last: dma("y", T.gr[:, :], T[LRn][0:128:16, C:], [R(LRn, C, 1152)], [])
        tt(R(XN, 768, 1536), R("H", 0, 1536, 1, R("mnU", 0, 48)), R(X, 768, 1536), OP.add)
        quant("q_x", HALF, C, XN, HALF)
        if k == 0:
            for b in range(4): quant("q_e", 128 * b, 128 * b + 128, "E", 0, 3 - b)
        if last: quant("q_v", 0, 128, "vt", 0)

        def finish(a):
            o = bank(a > 0, HALF)
            mm(o, "q_v", 0, "q_x", a, HALF)
            act(R("yS", a, a + HALF), o, ACT.Copy)
            dma("y" if a else "s", T.y[:, a:a + HALF], T.yS[:, a:a + HALF], [R("yS", a, a + HALF)], [])
            dma("y", T.oc[:, 4 * a:4 * a + 4 * HALF], T.q_x[:, a:a + HALF].bitcast(dt.uint8), [R("q_x", a, a + HALF)], [])
            for i in range(4):
                dma("y" if a or i < 2 else "s", T.osc[4 * i:4 * i + 4, a:a + HALF], T.q_xs[32 * i:32 * i + 4, a:a + HALF], [R("q_x", a, a + HALF)], [])
        if not last:
            scores(HALF, C, (0, 1))
            sign1(HALF, C)
            act(R("XYh", 2304, 3072), R("H", 0, 1536, 1, R("mnU", 0, 48)), ACT.Copy, 0.5)
            halves(768)
        else:
            finish(HALF)
        for b in range(4):
            mm(R("psH", 512 * b, 512 * b + HALF), "q_e", 128 * b, "cin%d" % k, 0, HALF, "sin%d" % k)
        if not last:
            scores(HALF, C, (2, 3))
            sign2(HALF, C)
            turns2(HALF, C)
        for b in range(4):
            tt(R(XN, b, 768, 4), R(X, b, 768, 4), R("psH", 512 * b, 512 * b + HALF), OP.add)
        quant("q_x", 0, HALF, XN, 0)
        if last: finish(0)
        else:
            for a in range(0, 24, OPT["lpn"]): scatter(k + 1, a, a + OPT["lpn"])
            parents(k + 1)
            for b in range(4): act(R("XYh", 1536 + b, 2304, 4), R("psH", 512 * b, 512 * b + HALF), ACT.Copy, 0.5)
            halves(0)
    emit()
